import numpy as np
import ml_dtypes


def mxq(x, axis, fmt="e4m3"):
    dtype, down = {"e4m3": (ml_dtypes.float8_e4m3fn, 7), "e5m2": (ml_dtypes.float8_e5m2, 14)}[fmt]
    v = np.moveaxis(np.asarray(x, np.float32).astype(ml_dtypes.bfloat16).astype(np.float64), axis, -1)
    blocks = v.reshape(v.shape[:-1] + (-1, 32))
    amax = np.abs(blocks).max(-1, keepdims=True)
    byte = np.maximum(np.where(amax > 0, np.frexp(amax)[1] - 1 + 127, 0) - down, 1)
    scale = np.exp2(byte - 127.0)
    codes = (blocks / scale).astype(np.float32).astype(dtype).astype(np.float64)
    return np.moveaxis((codes * scale).reshape(v.shape), -1, axis)


WIDE = False


def mx_kscale(k):
    if not WIDE:
        return np.ones(k)
    levels = np.array([10, -10, 5, -5, 0])
    if k % 512:
        return np.exp2(np.random.permutation(np.resize(levels, k // 32))).repeat(32)
    a = np.empty((k // 512, 16))
    for p in range(k // 512):
        a[p, :8] = np.random.permutation(np.resize(levels, 8))
        for g in range(8):
            far = levels[np.abs(levels - a[p, g]) >= 10]
            a[p, g + 8] = far[np.random.randint(len(far))]
    return np.exp2(a.ravel()).repeat(32)


def f64(x):
    return np.asarray(x).astype(np.float64)


def striped(idx):
    return np.tile(idx.reshape(-1, 16).T, (8, 1)).astype(np.uint16)


def unstriped(offs):
    return offs[:16].T.reshape(-1).astype(np.int64)


E2M1 = np.array([0.0, 0.5, 1.0, 1.5, 2.0, 3.0, 4.0, 6.0, -0.0, -0.5, -1.0, -1.5, -2.0, -3.0, -4.0, -6.0])


def pack_weight(w, fmt):
    k, n = w.shape
    w = f64(np.asarray(w, np.float32).astype(ml_dtypes.bfloat16)).reshape(k // 32, 32, n)
    amax = np.abs(w).max(1)
    if fmt == "e4m3":
        byte = np.frexp(amax)[1] - 1 + 127 - 7
    else:
        mant, ex = np.frexp(amax / 6.0)
        byte = np.where(mant > 0.5, ex, ex - 1) + 127
    byte = np.clip(np.where(amax > 0, byte, 1), 1, 254)
    scaled = (w * np.exp2(127.0 - byte)[:, None, :]).reshape(k, n).astype(np.float32)
    by_word = np.ascontiguousarray(scaled.reshape(k // 512, 128, 4, n).transpose(0, 1, 3, 2))
    if fmt == "e4m3":
        words = by_word.astype(ml_dtypes.float8_e4m3fn).view(np.uint8)
    else:
        c = by_word.astype(ml_dtypes.float4_e2m1fn).view(np.uint8) & 0xF
        words = (c[..., 0::2] | (c[..., 1::2] << 4)).reshape(k // 512, 128, 2 * n)
    return np.ascontiguousarray(words), np.ascontiguousarray(byte.astype(np.uint8).reshape(k // 512, 16, n))


def unpack_weight(words, scales, fmt):
    g, _, n = scales.shape
    words = np.ascontiguousarray(words).reshape(g, 128, n, -1)
    if fmt == "e4m3":
        vals = words.view(ml_dtypes.float8_e4m3fn).astype(np.float64)
    else:
        nib = np.empty((g, 128, n, 4), np.uint8)
        nib[..., 0::2] = words & 0xF
        nib[..., 1::2] = words >> 4
        vals = E2M1[nib]
    vals = vals * np.repeat(np.exp2(scales.astype(np.float64) - 127.0), 8, axis=1)[..., None]
    return vals.transpose(0, 1, 3, 2).reshape(g * 512, n)


def gelu(v):
    return 0.5 * v * (1.0 + np.tanh(np.sqrt(2.0 / np.pi) * (v + 0.044715 * v**3)))


def bf(x):
    return np.asarray(x, np.float32).astype(ml_dtypes.bfloat16)


def planes(Y):
    n, m = Y.shape
    b = f64(bf(Y)).reshape(n // 32, 32, m)
    amax = np.abs(b).max(1)
    byte = np.clip(np.where(amax > 0, np.frexp(amax)[1] - 1 + 127 - 7, 1), 1, 254)
    codes = (b * np.exp2(127.0 - byte)[:, None, :]).reshape(n, m).astype(np.float32).astype(ml_dtypes.float8_e4m3fn).view(np.uint8)
    words = codes.reshape(n // 512, 128, 4, m).transpose(0, 1, 3, 2)
    return np.ascontiguousarray(words), np.ascontiguousarray(byte.astype(np.uint8).reshape(n // 512, 16, m))


K, T, S, H, N = 1024, 2048, 1024, 1024, 512

def setup_inputs():
    n = np.random.standard_normal
    s = mx_kscale(K)[:, None]
    u = mx_kscale(H)[:, None]
    tab_words, tab_scales = pack_weight(n((K, T)) * s, "e4m3")
    w1_words, w1_scales = pack_weight(0.45 * n((K, H)) / np.sqrt(K) / s, "e4m3")
    w3_words, w3_scales = pack_weight(n((H, N)) / np.sqrt(H) / u, "e2m1")
    return {
        "tab_words": tab_words, "tab_scales": tab_scales,
        "offs": striped(np.random.permutation(T)[:S]),
        "offs2": striped(np.random.permutation(S)),
        "w1_words": w1_words, "w1_scales": w1_scales,
        "w2": (1.5 * n((H, N)) / np.sqrt(H) / u).astype(np.float32),
        "w3_words": w3_words, "w3_scales": w3_scales,
        "amp": (np.exp(0.3 * n((H, S))) * u).astype(np.float32),
        "gc": (np.exp(0.3 * n(H)) * u[:, 0]).astype(np.float32),
        "wgo": np.exp(0.3 * n((128, S))).astype(np.float32),
        "x0": (np.exp(0.3 * n((N, S))) * np.exp(0.8 * n(N))[:, None]).astype(np.float32),
    }

def reference(tab_words, tab_scales, offs, offs2, w1_words, w1_scales, w2, w3_words, w3_scales, amp, gc, wgo, x0):
    v = unpack_weight(tab_words, tab_scales, "e4m3")[:, unstriped(offs)]
    W1 = unpack_weight(w1_words, w1_scales, "e4m3")
    W2 = mxq(f64(w2), 0, "e4m3")
    W3 = unpack_weight(w3_words, w3_scales, "e2m1")
    a = W1.T @ v
    hs = mxq(np.sin(a) * f64(amp), 0, "e4m3")
    hc = mxq(np.cos(a) * f64(gc)[:, None], 0, "e4m3")
    d = W2.T @ hs + W3.T @ hc
    page = np.zeros((N, S))
    page[:, unstriped(offs2)] = np.tile(f64(wgo), (N // 128, 1)) * d
    y = page * f64(x0)
    words, scales = planes(y)
    return y, words, scales

@@ -1,0 +1,301 @@
+import math
+from contextlib import ExitStack
+
+import concourse.mybir as mybir
+from concourse.masks import make_identity
+
+K, T, S, H, N = 1024, 2048, 1024, 1024, 512
+FLOPS = 2 * K * H * S + 2 * 2 * H * N * S
+
+F32 = mybir.dt.float32
+BF16 = mybir.dt.bfloat16
+I32 = mybir.dt.int32
+U32 = mybir.dt.uint32
+U16 = mybir.dt.uint16
+U8 = mybir.dt.uint8
+FP8X4 = mybir.dt.float8_e4m3fn_x4
+FP4X4 = mybir.dt.float4_e2m1fn_x4
+ACT = mybir.ActivationFunctionType
+ALU = mybir.AluOpType
+
+P = 128
+PACK = 4
+G = 2
+TOK = 128
+TILES = S // TOK
+GATHER = 256
+AMP_COLS = 256
+WGO_COLS = 512
+
+TURN_BASE = 98304.0
+TURN_BITS = 1203765248.0
+TURN_STEP = 128.0
+
+
+def tile_list_tide_sorted_growth_kernel(
+    tc, tab_words, tab_scales, offs, offs2, w1_words, w1_scales, w2, w3_words, w3_scales, amp, gc, wgo, x0,
+    out_0, out_1, out_2,
+):
+    nc = tc.nc
+    with ExitStack() as ctx:
+        lists = ctx.enter_context(tc.tile_pool(name="lists", bufs=1))
+        keep = ctx.enter_context(tc.tile_pool(name="keep", bufs=1))
+        ring = ctx.enter_context(tc.tile_pool(name="ring", bufs=2))
+        psum = ctx.enter_context(tc.psum_pool(name="psum", bufs=2))
+
+        idx = lists.tile([P, S // 16], U16, name="idx")
+        idx2 = lists.tile([P, S // 16], U16, name="idx2")
+
+        tab_w = [keep.tile([P, T], U32, name="tab_w%d" % a, align_bytes=64) for a in range(G)]
+        tab_s = keep.tile([P, T], U8, name="tab_s", align_bytes=64)
+        w1_w = [keep.tile([P, G, 512], U32, name="w1_w%d" % g, align_bytes=64) for g in range(G)]
+        w1_s = keep.tile([P, H], U8, name="w1_s", align_bytes=64)
+        w3_s_raw = keep.tile([P, G, N], U8, name="w3_s_raw", align_bytes=64)
+        ident = keep.tile([P, P], F32, name="ident")
+        minus_base = keep.tile([P, P], F32, name="minus_base")
+
+        nc.gpsimd.memset(tab_s[:].bitcast(I32), 0)
+        nc.gpsimd.memset(w1_s[:].bitcast(I32), 0)
+        make_identity(nc, ident[:])
+        nc.vector.memset(minus_base[:], -TURN_BASE)
+        nc.vector.memset(w3_s_raw[:].rearrange("p g n -> p (g n)").bitcast(I32), 0)
+
+        def load_words(dst, words):
+            nc.sync.dma_start(out=dst.bitcast(I32), in_=words.rearrange("p c i -> p (c i)").bitcast(I32))
+
+        nc.sync.dma_start(idx[:], offs)
+        load_words(tab_w[0][:], tab_words[0])
+        for q in range(4):
+            nc.sync.dma_start(
+                out=tab_s[32 * q : 32 * q + 8, :].bitcast(I32), in_=tab_scales[:, 4 * q : 4 * q + 4, :].bitcast(I32)
+            )
+        load_words(tab_w[1][:], tab_words[1])
+
+        def load_w1(g):
+            nc.sync.dma_start(
+                out=w1_w[g][:].bitcast(I32),
+                in_=w1_words[:, :, 512 * g : 512 * (g + 1), :].rearrange("a p c i -> p a (c i)").bitcast(I32),
+            )
+
+        load_w1(0)
+        for q in range(4):
+            nc.sync.dma_start(
+                out=w1_s[32 * q : 32 * q + 8, :].bitcast(I32), in_=w1_scales[:, 4 * q : 4 * q + 4, :].bitcast(I32)
+            )
+        load_w1(1)
+
+        amp_rows = amp.rearrange("(g p t) j -> g p t j", g=G, t=PACK)
+        amp_t = {}
+
+        def load_amp(quarter):
+            for g in range(G):
+                piece = keep.tile([P, PACK, AMP_COLS], F32, name="amp%d_%d" % (quarter, g))
+                nc.sync.dma_start(out=piece[:], in_=amp_rows[g][:, :, quarter * AMP_COLS : (quarter + 1) * AMP_COLS])
+                amp_t[quarter, g] = piece
+
+        wgo_rows = wgo.rearrange("(q t) j -> q t j", t=PACK)
+        wgo_t = {}
+
+        def load_wgo(half):
+            piece = keep.tile([P, PACK, WGO_COLS], F32, name="wgo%d" % half)
+            for q in range(4):
+                nc.sync.dma_start(
+                    out=piece[32 * q : 32 * q + 32], in_=wgo_rows[:, :, half * WGO_COLS : (half + 1) * WGO_COLS]
+                )
+            wgo_t[half] = piece
+
+        load_amp(0)
+        gc_t = keep.tile([P, G, PACK], F32, name="gc_t")
+        nc.sync.dma_start(out=gc_t[:], in_=gc.rearrange("(g p t) -> p g t", g=G, t=PACK))
+        w2_raw = [keep.tile([P, PACK, N], F32, name="w2_raw%d" % g) for g in range(G)]
+        for g in range(G):
+            nc.sync.dma_start(out=w2_raw[g][:], in_=w2.rearrange("(g p j) n -> g p j n", g=G, j=PACK)[g])
+        w3_w_raw = keep.tile([P, G, 2 * N], U8, name="w3_w_raw", align_bytes=64)
+        nc.sync.dma_start(out=w3_w_raw[:].bitcast(I32), in_=w3_words.rearrange("g p b -> p g b").bitcast(I32))
+        for q in range(4):
+            nc.sync.dma_start(
+                out=w3_s_raw[32 * q : 32 * q + 4].bitcast(I32),
+                in_=w3_scales[:, 4 * q : 4 * q + 4, :].rearrange("g r n -> r g n").bitcast(I32),
+            )
+        nc.sync.dma_start(idx2[:], offs2)
+        load_wgo(0)
+        load_amp(1)
+        load_amp(2)
+        load_wgo(1)
+        load_amp(3)
+        y = [keep.tile([P, S], F32, name="y%d" % t) for t in range(PACK)]
+        for t in range(PACK):
+            nc.sync.dma_start(out=y[t][:], in_=x0.rearrange("(p t) m -> t p m", t=PACK)[t])
+
+        v_w = {}
+        v_s = {}
+        for c in range(S // GATHER):
+            offsets = idx[:, c * GATHER // 16 : (c + 1) * GATHER // 16]
+            for a in range(G):
+                words = keep.tile([P, GATHER], U32, name="v_w%d_%d" % (c, a), align_bytes=64)
+                nc.vector.tensor_copy(out=words[:], in_=tab_w[a][:].indirect(offsets))
+                v_w[c, a] = words
+            planes = keep.tile([P, GATHER], U8, name="v_s%d" % c, align_bytes=64)
+            nc.vector.tensor_copy(out=planes[:], in_=tab_s[:].indirect(offsets))
+            v_s[c] = planes
+
+        w2_w = keep.tile([P, G, N], U32, name="w2_w", align_bytes=64)
+        w2_s = keep.tile([P, G, N], U8, name="w2_s", align_bytes=64)
+        for g in range(G):
+            w2_b = keep.tile([P, PACK, P, PACK], BF16, name="w2_b%d" % g, align_bytes=64)
+            nc.vector.tensor_copy(
+                out=w2_b[:].rearrange("p t m j -> p m t j"), in_=w2_raw[g][:].rearrange("p j (m t) -> p m t j", t=PACK)
+            )
+            nc.vector.quantize_mx(
+                out=w2_w[:, g, :].bitcast(FP8X4), scales=w2_s[:, g, :], in_=w2_b[:].rearrange("p t m j -> p (t m j)")
+            )
+        w3_w = keep.tile([P, G, 2 * N], U8, name="w3_w", align_bytes=64)
+        w3_s = keep.tile([P, G, N], U8, name="w3_s", align_bytes=64)
+        nc.vector.tensor_copy(
+            out=w3_w[:].bitcast(U16).rearrange("p g (t m) -> p g t m", t=PACK),
+            in_=w3_w_raw[:].bitcast(U16).rearrange("p g (m t) -> p g t m", t=PACK),
+        )
+        nc.vector.tensor_copy(
+            out=w3_s[:].rearrange("p g (t m) -> p g t m", t=PACK),
+            in_=w3_s_raw[:].rearrange("p g (m t) -> p g t m", t=PACK),
+        )
+
+        page = [keep.tile([P, S], F32, name="page%d" % t) for t in range(PACK)]
+
+        def angles(i):
+            c, lo = divmod(i * TOK, GATHER)
+            turns = ring.tile([P, G, PACK, P], F32, name="turns")
+            whole = ring.tile([P, G, PACK, P], U32, name="whole")
+            for g in range(G):
+                a_t = psum.tile([P, 512], F32, name="a_t", bufs=2)
+                for a in range(G):
+                    nc.tensor.matmul_mx(
+                        out=a_t[:],
+                        lhsT=v_w[c, a][:, lo : lo + TOK].bitcast(FP8X4),
+                        lhsT_scale=v_s[c][4 * a :, lo : lo + TOK],
+                        rhs=w1_w[g][:, a, :].bitcast(FP8X4),
+                        rhs_scale=w1_s[4 * a :, 512 * g : 512 * (g + 1)],
+                        start=(a == 0),
+                        stop=(a == G - 1),
+                    )
+                nc.scalar.activation(
+                    out=turns[:, g], in_=a_t[:].rearrange("j (p t) -> j t p", t=PACK), func=ACT.Copy,
+                    scale=1.0 / (2.0 * math.pi),
+                )
+            nc.scalar.activation(
+                out=whole[:].rearrange("j g t p -> j (g t p)"), in_=turns[:].rearrange("j g t p -> j (g t p)"),
+                func=ACT.Copy, scale=-TURN_STEP, bias=TURN_BITS,
+            )
+            banks = []
+            for g in range(G):
+                frac = psum.tile([P, PACK, TOK], F32, name="frac", bufs=4)
+                for t in range(PACK):
+                    terms = (minus_base[:], whole[:, g, t, :].bitcast(F32), turns[:, g, t, :])
+                    for s, term in enumerate(terms):
+                        nc.tensor.matmul(
+                            out=frac[:, t, :], lhsT=term, rhs=ident[:], is_transpose=True,
+                            start=(s == 0), stop=(s == len(terms) - 1),
+                        )
+                banks.append(frac)
+            return banks
+
+        def waves(banks):
+            sine = ring.tile([P, G, PACK, TOK], F32, name="sine")
+            cosine = ring.tile([P, G, TOK, PACK], F32, name="cosine")
+            folded = ring.tile([P, G, TOK * PACK], F32, name="folded")
+            for g in range(G):
+                nc.scalar.activation(out=sine[:, g], in_=banks[g][:], func=ACT.Sin, scale=2.0 * math.pi)
+                nc.scalar.activation(
+                    out=folded[:, g].rearrange("p (j t) -> p j t", t=PACK),
+                    in_=banks[g][:].rearrange("p t j -> p j t"), func=ACT.Abs,
+                )
+            nc.scalar.activation(
+                out=cosine[:].rearrange("p g j t -> p (g j t)"), in_=folded[:].rearrange("p g e -> p (g e)"),
+                func=ACT.Sin, scale=-2.0 * math.pi, bias=math.pi / 2.0,
+            )
+            return sine, cosine, folded
+
+        def growth(i, sine, cosine):
+            quarter, lo = divmod(i * TOK, AMP_COLS)
+            h_b = ring.tile([P, 2 * G, TOK, PACK], BF16, name="h_b", align_bytes=64)
+            for g in range(G):
+                nc.vector.tensor_tensor(
+                    out=h_b[:, g].rearrange("p (c i) t -> p c t i", i=4),
+                    in0=sine[:, g].rearrange("p t (c i) -> p c t i", i=4),
+                    in1=amp_t[quarter, g][:, :, lo : lo + TOK].rearrange("p t (c i) -> p c t i", i=4),
+                    op=ALU.mult,
+                )
+            nc.vector.tensor_tensor(
+                out=h_b[:, G:], in0=cosine[:], in1=gc_t[:].unsqueeze(2).to_broadcast([P, G, TOK, PACK]), op=ALU.mult
+            )
+            h_w = ring.tile([P, 2 * G * TOK], U32, name="h_w", align_bytes=64)
+            h_s = ring.tile([P, 2 * G * TOK], U8, name="h_s", align_bytes=64)
+            nc.vector.quantize_mx(
+                out=h_w[:].bitcast(FP8X4), scales=h_s[:], in_=h_b[:].rearrange("p o j t -> p (o j t)")
+            )
+            d = psum.tile([P, PACK, TOK], F32, name="d", bufs=2)
+            for t in range(PACK):
+                cols = slice(t * P, (t + 1) * P)
+                for o in range(2 * G):
+                    g = o % G
+                    if o < G:
+                        weights, scales = w2_w[:, g, cols].bitcast(FP8X4), w2_s[:, g, cols]
+                    else:
+                        weights, scales = w3_w[:, g, 2 * t * P : 2 * (t + 1) * P].bitcast(FP4X4), w3_s[:, g, cols]
+                    nc.tensor.matmul_mx(
+                        out=d[:, t, :],
+                        lhsT=weights,
+                        lhsT_scale=scales,
+                        rhs=h_w[:, o * TOK : (o + 1) * TOK].bitcast(FP8X4),
+                        rhs_scale=h_s[:, o * TOK : (o + 1) * TOK],
+                        start=(o == 0),
+                        stop=(o == 2 * G - 1),
+                    )
+            return d
+
+        def place(i, d, scratch):
+            half, lo = divmod(i * TOK, WGO_COLS)
+            d_sb = scratch.rearrange("p (t j) -> p t j", t=PACK)
+            nc.scalar.copy(out=d_sb, in_=d[:])
+            offsets = idx2[:, i * TOK // 16 : (i + 1) * TOK // 16]
+            for t in range(PACK):
+                nc.vector.tensor_tensor(
+                    out=page[t][:].indirect(offsets), in0=d_sb[:, t, :], in1=wgo_t[half][:, t, lo : lo + TOK],
+                    op=ALU.mult,
+                )
+
+        banks = {0: angles(0)}
+        sums = {}
+        for i in range(TILES):
+            if i + 1 < TILES:
+                banks[i + 1] = angles(i + 1)
+            sine, cosine, folded = waves(banks[i])
+            sums[i] = growth(i, sine, cosine)
+            if i >= 1:
+                place(i - 1, sums[i - 1], folded[:, 0])
+        place(TILES - 1, sums[TILES - 1], folded[:, 1])
+
+        y_all = keep.tile([P, PACK, S], F32, name="y_all")
+        for t in range(PACK):
+            nc.vector.tensor_tensor(out=y_all[:, t, :], in0=page[t][:], in1=y[t][:], op=ALU.mult)
+            nc.sync.dma_start(out=out_0.rearrange("(p t) m -> t p m", t=PACK)[t], in_=y_all[:, t, :])
+        y_w = keep.tile([P, S], U32, name="y_w", align_bytes=64)
+        y_s = keep.tile([P, S], U8, name="y_s", align_bytes=64)
+        for lo, hi, engine in ((0, 256, "scalar"), (512, 1024, "vector"), (256, 512, "vector")):
+            y_b = keep.tile([P, hi - lo, PACK], BF16, name="y_b%d" % lo, align_bytes=64)
+            dst = y_b[:].rearrange("p (c i) t -> p c t i", i=4)
+            src = y_all[:, :, lo:hi].rearrange("p t (c i) -> p c t i", i=4)
+            if engine == "scalar":
+                nc.scalar.copy(out=dst, in_=src)
+            else:
+                nc.vector.tensor_copy(out=dst, in_=src)
+            nc.vector.quantize_mx(
+                out=y_w[:, lo:hi].bitcast(FP8X4), scales=y_s[:, lo:hi], in_=y_b[:].rearrange("p c t -> p (c t)")
+            )
+            nc.sync.dma_start(
+                out=out_1[0][:, lo:hi, :].rearrange("p c i -> p (c i)").bitcast(I32), in_=y_w[:, lo:hi].bitcast(I32)
+            )
+        for q in range(4):
+            nc.scalar.dma_start(
+                out=out_2[0][4 * q : 4 * q + 4, :].bitcast(I32), in_=y_s[32 * q : 32 * q + 4, :].bitcast(I32)
+            )

@@ -26,6 +26,8 @@ TILES = S // TOK
 GATHER = 256
 AMP_COLS = 256
 WGO_COLS = 512
+LAG = 2
+ROUNDED_ON_VECTOR = (1, 2)
 
 TURN_BASE = 98304.0
 TURN_BITS = 1203765248.0
@@ -63,26 +65,25 @@ def tile_list_tide_sorted_growth_kernel(
         def load_words(dst, words):
             nc.sync.dma_start(out=dst.bitcast(I32), in_=words.rearrange("p c i -> p (c i)").bitcast(I32))
 
+        def load_scales(dst, scales, q):
+            nc.sync.dma_start(
+                out=dst[32 * q : 32 * q + 8, :].bitcast(I32), in_=scales[:, 4 * q : 4 * q + 4, :].bitcast(I32)
+            )
+
         nc.sync.dma_start(idx[:], offs)
         load_words(tab_w[0][:], tab_words[0])
         for q in range(4):
-            nc.sync.dma_start(
-                out=tab_s[32 * q : 32 * q + 8, :].bitcast(I32), in_=tab_scales[:, 4 * q : 4 * q + 4, :].bitcast(I32)
-            )
+            load_scales(tab_s, tab_scales, q)
+        for q in range(2):
+            load_scales(w1_s, w1_scales, q)
         load_words(tab_w[1][:], tab_words[1])
-
-        def load_w1(g):
+        for q in range(2, 4):
+            load_scales(w1_s, w1_scales, q)
+        for g in range(G):
             nc.sync.dma_start(
                 out=w1_w[g][:].bitcast(I32),
                 in_=w1_words[:, :, 512 * g : 512 * (g + 1), :].rearrange("a p c i -> p a (c i)").bitcast(I32),
             )
-
-        load_w1(0)
-        for q in range(4):
-            nc.sync.dma_start(
-                out=w1_s[32 * q : 32 * q + 8, :].bitcast(I32), in_=w1_scales[:, 4 * q : 4 * q + 4, :].bitcast(I32)
-            )
-        load_w1(1)
 
         amp_rows = amp.rearrange("(g p t) j -> g p t j", g=G, t=PACK)
         amp_t = {}
@@ -105,11 +106,11 @@ def tile_list_tide_sorted_growth_kernel(
             wgo_t[half] = piece
 
         load_amp(0)
-        gc_t = keep.tile([P, G, PACK], F32, name="gc_t")
-        nc.sync.dma_start(out=gc_t[:], in_=gc.rearrange("(g p t) -> p g t", g=G, t=PACK))
         w2_raw = [keep.tile([P, PACK, N], F32, name="w2_raw%d" % g) for g in range(G)]
         for g in range(G):
             nc.sync.dma_start(out=w2_raw[g][:], in_=w2.rearrange("(g p j) n -> g p j n", g=G, j=PACK)[g])
+        gc_t = keep.tile([P, G, PACK], F32, name="gc_t")
+        nc.sync.dma_start(out=gc_t[:], in_=gc.rearrange("(g p t) -> p g t", g=G, t=PACK))
         w3_w_raw = keep.tile([P, G, 2 * N], U8, name="w3_w_raw", align_bytes=64)
         nc.sync.dma_start(out=w3_w_raw[:].bitcast(I32), in_=w3_words.rearrange("g p b -> p g b").bitcast(I32))
         for q in range(4):
@@ -123,9 +124,10 @@ def tile_list_tide_sorted_growth_kernel(
         load_amp(2)
         load_wgo(1)
         load_amp(3)
-        y = [keep.tile([P, S], F32, name="y%d" % t) for t in range(PACK)]
-        for t in range(PACK):
-            nc.sync.dma_start(out=y[t][:], in_=x0.rearrange("(p t) m -> t p m", t=PACK)[t])
+        halves = (slice(0, S // 2), slice(S // 2, S))
+        y = [keep.tile([P, PACK, S // 2], F32, name="y%d" % h) for h in range(2)]
+        for h, cols in enumerate(halves):
+            nc.sync.dma_start(out=y[h][:], in_=x0.rearrange("(p t) m -> p t m", t=PACK)[:, :, cols])
 
         v_w = {}
         v_s = {}
@@ -141,31 +143,32 @@ def tile_list_tide_sorted_growth_kernel(
 
         w2_w = keep.tile([P, G, N], U32, name="w2_w", align_bytes=64)
         w2_s = keep.tile([P, G, N], U8, name="w2_s", align_bytes=64)
-        for g in range(G):
-            w2_b = keep.tile([P, PACK, P, PACK], BF16, name="w2_b%d" % g, align_bytes=64)
-            nc.vector.tensor_copy(
-                out=w2_b[:].rearrange("p t m j -> p m t j"), in_=w2_raw[g][:].rearrange("p j (m t) -> p m t j", t=PACK)
-            )
-            nc.vector.quantize_mx(
-                out=w2_w[:, g, :].bitcast(FP8X4), scales=w2_s[:, g, :], in_=w2_b[:].rearrange("p t m j -> p (t m j)")
-            )
         w3_w = keep.tile([P, G, 2 * N], U8, name="w3_w", align_bytes=64)
         w3_s = keep.tile([P, G, N], U8, name="w3_s", align_bytes=64)
-        nc.vector.tensor_copy(
-            out=w3_w[:].bitcast(U16).rearrange("p g (t m) -> p g t m", t=PACK),
-            in_=w3_w_raw[:].bitcast(U16).rearrange("p g (m t) -> p g t m", t=PACK),
-        )
-        nc.vector.tensor_copy(
-            out=w3_s[:].rearrange("p g (t m) -> p g t m", t=PACK),
-            in_=w3_s_raw[:].rearrange("p g (m t) -> p g t m", t=PACK),
-        )
+
+        def deal_weights():
+            for g in range(G):
+                w2_b = keep.tile([P, PACK, P, PACK], BF16, name="w2_b%d" % g, align_bytes=64)
+                nc.vector.tensor_copy(
+                    out=w2_b[:].rearrange("p t m j -> p m t j"), in_=w2_raw[g][:].rearrange("p j (m t) -> p m t j", t=PACK)
+                )
+                nc.vector.quantize_mx(
+                    out=w2_w[:, g, :].bitcast(FP8X4), scales=w2_s[:, g, :], in_=w2_b[:].rearrange("p t m j -> p (t m j)")
+                )
+            nc.vector.tensor_copy(
+                out=w3_w[:].bitcast(U16).rearrange("p g (t m) -> p g t m", t=PACK),
+                in_=w3_w_raw[:].bitcast(U16).rearrange("p g (m t) -> p g t m", t=PACK),
+            )
+            nc.vector.tensor_copy(
+                out=w3_s[:].rearrange("p g (t m) -> p g t m", t=PACK),
+                in_=w3_s_raw[:].rearrange("p g (m t) -> p g t m", t=PACK),
+            )
 
         page = [keep.tile([P, S], F32, name="page%d" % t) for t in range(PACK)]
 
         def angles(i):
             c, lo = divmod(i * TOK, GATHER)
-            turns = ring.tile([P, G, PACK, P], F32, name="turns")
-            whole = ring.tile([P, G, PACK, P], U32, name="whole")
+            banks = []
             for g in range(G):
                 a_t = psum.tile([P, 512], F32, name="a_t", bufs=2)
                 for a in range(G):
@@ -178,14 +181,28 @@ def tile_list_tide_sorted_growth_kernel(
                         start=(a == 0),
                         stop=(a == G - 1),
                     )
+                banks.append(a_t)
+            return banks
+
+        def to_turns(i, banks):
+            turns = ring.tile([P, G, PACK, P], F32, name="turns", bufs=3)
+            for g in range(G):
                 nc.scalar.activation(
-                    out=turns[:, g], in_=a_t[:].rearrange("j (p t) -> j t p", t=PACK), func=ACT.Copy,
+                    out=turns[:, g], in_=banks[g][:].rearrange("j (p t) -> j t p", t=PACK), func=ACT.Copy,
                     scale=1.0 / (2.0 * math.pi),
                 )
-            nc.scalar.activation(
-                out=whole[:].rearrange("j g t p -> j (g t p)"), in_=turns[:].rearrange("j g t p -> j (g t p)"),
-                func=ACT.Copy, scale=-TURN_STEP, bias=TURN_BITS,
-            )
+            whole = ring.tile([P, G, PACK, P], U32, name="whole", bufs=3)
+            src = turns[:].rearrange("j g t p -> j (g t p)")
+            dst = whole[:].rearrange("j g t p -> j (g t p)")
+            if i in ROUNDED_ON_VECTOR:
+                nc.vector.tensor_scalar(
+                    out=dst.bitcast(I32), in0=src, scalar1=-TURN_STEP, scalar2=TURN_BITS, op0=ALU.mult, op1=ALU.add
+                )
+            else:
+                nc.scalar.activation(out=dst, in_=src, func=ACT.Copy, scale=-TURN_STEP, bias=TURN_BITS)
+            return turns, whole
+
+        def reduce_turns(turns, whole):
             banks = []
             for g in range(G):
                 frac = psum.tile([P, PACK, TOK], F32, name="frac", bufs=4)
@@ -215,7 +232,7 @@ def tile_list_tide_sorted_growth_kernel(
             )
             return sine, cosine, folded
 
-        def growth(i, sine, cosine):
+        def weigh(i, sine, cosine):
             quarter, lo = divmod(i * TOK, AMP_COLS)
             h_b = ring.tile([P, 2 * G, TOK, PACK], BF16, name="h_b", align_bytes=64)
             for g in range(G):
@@ -233,6 +250,9 @@ def tile_list_tide_sorted_growth_kernel(
             nc.vector.quantize_mx(
                 out=h_w[:].bitcast(FP8X4), scales=h_s[:], in_=h_b[:].rearrange("p o j t -> p (o j t)")
             )
+            return (h_w, h_s), h_b[:].rearrange("p o j t -> p (o j t)").bitcast(F32)
+
+        def growth(h_w, h_s):
             d = psum.tile([P, PACK, TOK], F32, name="d", bufs=2)
             for t in range(PACK):
                 cols = slice(t * P, (t + 1) * P)
@@ -253,10 +273,13 @@ def tile_list_tide_sorted_growth_kernel(
                     )
             return d
 
-        def place(i, d, scratch):
-            half, lo = divmod(i * TOK, WGO_COLS)
+        def evacuate(d, scratch):
             d_sb = scratch.rearrange("p (t j) -> p t j", t=PACK)
             nc.scalar.copy(out=d_sb, in_=d[:])
+            return d_sb
+
+        def place(i, d_sb):
+            half, lo = divmod(i * TOK, WGO_COLS)
             offsets = idx2[:, i * TOK // 16 : (i + 1) * TOK // 16]
             for t in range(PACK):
                 nc.vector.tensor_tensor(
@@ -264,36 +287,52 @@ def tile_list_tide_sorted_growth_kernel(
                     op=ALU.mult,
                 )
 
-        banks = {0: angles(0)}
-        sums = {}
+        turns = {i: to_turns(i, angles(i)) for i in range(2)}
+        fracs = {0: reduce_turns(*turns[0])}
+        codes, sums = {}, {}
         for i in range(TILES):
+            if i + 2 < TILES:
+                a_banks = angles(i + 2)
             if i + 1 < TILES:
-                banks[i + 1] = angles(i + 1)
-            sine, cosine, folded = waves(banks[i])
-            sums[i] = growth(i, sine, cosine)
+                fracs[i + 1] = reduce_turns(*turns[i + 1])
             if i >= 1:
-                place(i - 1, sums[i - 1], folded[:, 0])
-        place(TILES - 1, sums[TILES - 1], folded[:, 1])
+                sums[i - 1] = growth(*codes[i - 1])
+            sine, cosine, folded = waves(fracs[i])
+            if i >= LAG:
+                d_sb = evacuate(sums[i - LAG], folded[:, 0])
+            if i + 2 < TILES:
+                turns[i + 2] = to_turns(i + 2, a_banks)
+            codes[i], spent = weigh(i, sine, cosine)
+            if i == 0:
+                deal_weights()
+            if i >= LAG:
+                place(i - LAG, d_sb)
+        sums[TILES - 1] = growth(*codes[TILES - 1])
+        for r, i in enumerate(range(TILES - LAG, TILES)):
+            place(i, evacuate(sums[i], spent[:, r * PACK * TOK : (r + 1) * PACK * TOK]))
 
-        y_all = keep.tile([P, PACK, S], F32, name="y_all")
-        for t in range(PACK):
-            nc.vector.tensor_tensor(out=y_all[:, t, :], in0=page[t][:], in1=y[t][:], op=ALU.mult)
-            nc.sync.dma_start(out=out_0.rearrange("(p t) m -> t p m", t=PACK)[t], in_=y_all[:, t, :])
         y_w = keep.tile([P, S], U32, name="y_w", align_bytes=64)
         y_s = keep.tile([P, S], U8, name="y_s", align_bytes=64)
-        for lo, hi, engine in ((0, 256, "scalar"), (512, 1024, "vector"), (256, 512, "vector")):
-            y_b = keep.tile([P, hi - lo, PACK], BF16, name="y_b%d" % lo, align_bytes=64)
-            dst = y_b[:].rearrange("p (c i) t -> p c t i", i=4)
-            src = y_all[:, :, lo:hi].rearrange("p t (c i) -> p c t i", i=4)
-            if engine == "scalar":
+        y_b = [keep.tile([P, S // 2, PACK], BF16, name="y_b%d" % h, align_bytes=64) for h in range(2)]
+        for h, cols in enumerate(halves):
+            for t in range(PACK):
+                nc.vector.tensor_tensor(out=y[h][:, t, :], in0=page[t][:, cols], in1=y[h][:, t, :], op=ALU.mult)
+            nc.sync.dma_start(
+                out=out_0.rearrange("(p t) m -> p t m", t=PACK)[:, :, cols], in_=y[h][:]
+            )
+            dst = y_b[h][:].rearrange("p (c i) t -> p c t i", i=4)
+            src = y[h][:].rearrange("p t (c i) -> p c t i", i=4)
+            if h == 0:
                 nc.scalar.copy(out=dst, in_=src)
             else:
                 nc.vector.tensor_copy(out=dst, in_=src)
+        for h in (1, 0):
+            cols = halves[h]
             nc.vector.quantize_mx(
-                out=y_w[:, lo:hi].bitcast(FP8X4), scales=y_s[:, lo:hi], in_=y_b[:].rearrange("p c t -> p (c t)")
+                out=y_w[:, cols].bitcast(FP8X4), scales=y_s[:, cols], in_=y_b[h][:].rearrange("p c t -> p (c t)")
             )
             nc.sync.dma_start(
-                out=out_1[0][:, lo:hi, :].rearrange("p c i -> p (c i)").bitcast(I32), in_=y_w[:, lo:hi].bitcast(I32)
+                out=out_1[0][:, cols, :].rearrange("p c i -> p (c i)").bitcast(I32), in_=y_w[:, cols].bitcast(I32)
             )
         for q in range(4):
             nc.scalar.dma_start(

@@ -20,14 +20,18 @@ ALU = mybir.AluOpType
 
 P = 128
 PACK = 4
+PASS = P * PACK
 G = 2
+QUADS = 4
 TOK = 128
 TILES = S // TOK
+LIST_COL = 16
+RUN = 4
 GATHER = 256
 AMP_COLS = 256
 WGO_COLS = 512
 LAG = 2
-ROUNDED_ON_VECTOR = (1, 2)
+ROUNDED_ON_VECTOR = (1, 2, 3)
 
 TURN_BASE = 98304.0
 TURN_BITS = 1203765248.0
@@ -45,12 +49,12 @@ def tile_list_tide_sorted_growth_kernel(
         ring = ctx.enter_context(tc.tile_pool(name="ring", bufs=2))
         psum = ctx.enter_context(tc.psum_pool(name="psum", bufs=2))
 
-        idx = lists.tile([P, S // 16], U16, name="idx")
-        idx2 = lists.tile([P, S // 16], U16, name="idx2")
+        idx = lists.tile([P, S // LIST_COL], U16, name="idx")
+        idx2 = lists.tile([P, S // LIST_COL], U16, name="idx2")
 
         tab_w = [keep.tile([P, T], U32, name="tab_w%d" % a, align_bytes=64) for a in range(G)]
         tab_s = keep.tile([P, T], U8, name="tab_s", align_bytes=64)
-        w1_w = [keep.tile([P, G, 512], U32, name="w1_w%d" % g, align_bytes=64) for g in range(G)]
+        w1_w = [keep.tile([P, H], U32, name="w1_w%d" % a, align_bytes=64) for a in range(G)]
         w1_s = keep.tile([P, H], U8, name="w1_s", align_bytes=64)
         w3_s_raw = keep.tile([P, G, N], U8, name="w3_s_raw", align_bytes=64)
         ident = keep.tile([P, P], F32, name="ident")
@@ -67,43 +71,40 @@ def tile_list_tide_sorted_growth_kernel(
 
         def load_scales(dst, scales, q):
             nc.sync.dma_start(
-                out=dst[32 * q : 32 * q + 8, :].bitcast(I32), in_=scales[:, 4 * q : 4 * q + 4, :].bitcast(I32)
+                out=dst[32 * q : 32 * q + 4 * G, :].bitcast(I32), in_=scales[:, 4 * q : 4 * q + 4, :].bitcast(I32)
             )
 
         nc.sync.dma_start(idx[:], offs)
         load_words(tab_w[0][:], tab_words[0])
-        for q in range(4):
+        for q in range(QUADS):
             load_scales(tab_s, tab_scales, q)
-        for q in range(2):
+        for q in range(QUADS // 2):
             load_scales(w1_s, w1_scales, q)
         load_words(tab_w[1][:], tab_words[1])
-        for q in range(2, 4):
+        for q in range(QUADS // 2, QUADS):
             load_scales(w1_s, w1_scales, q)
-        for g in range(G):
-            nc.sync.dma_start(
-                out=w1_w[g][:].bitcast(I32),
-                in_=w1_words[:, :, 512 * g : 512 * (g + 1), :].rearrange("a p c i -> p a (c i)").bitcast(I32),
-            )
+        for a in range(G):
+            load_words(w1_w[a][:], w1_words[a])
 
         amp_rows = amp.rearrange("(g p t) j -> g p t j", g=G, t=PACK)
         amp_t = {}
 
-        def load_amp(quarter):
+        def load_amp(part):
             for g in range(G):
-                piece = keep.tile([P, PACK, AMP_COLS], F32, name="amp%d_%d" % (quarter, g))
-                nc.sync.dma_start(out=piece[:], in_=amp_rows[g][:, :, quarter * AMP_COLS : (quarter + 1) * AMP_COLS])
-                amp_t[quarter, g] = piece
+                piece = keep.tile([P, PACK, AMP_COLS], F32, name="amp%d_%d" % (part, g))
+                nc.sync.dma_start(out=piece[:], in_=amp_rows[g][:, :, part * AMP_COLS : (part + 1) * AMP_COLS])
+                amp_t[part, g] = piece
 
         wgo_rows = wgo.rearrange("(q t) j -> q t j", t=PACK)
         wgo_t = {}
 
-        def load_wgo(half):
-            piece = keep.tile([P, PACK, WGO_COLS], F32, name="wgo%d" % half)
-            for q in range(4):
+        def load_wgo(part):
+            piece = keep.tile([P, PACK, WGO_COLS], F32, name="wgo%d" % part)
+            for q in range(QUADS):
                 nc.sync.dma_start(
-                    out=piece[32 * q : 32 * q + 32], in_=wgo_rows[:, :, half * WGO_COLS : (half + 1) * WGO_COLS]
+                    out=piece[32 * q : 32 * q + 32], in_=wgo_rows[:, :, part * WGO_COLS : (part + 1) * WGO_COLS]
                 )
-            wgo_t[half] = piece
+            wgo_t[part] = piece
 
         load_amp(0)
         w2_raw = [keep.tile([P, PACK, N], F32, name="w2_raw%d" % g) for g in range(G)]
@@ -113,7 +114,7 @@ def tile_list_tide_sorted_growth_kernel(
         nc.sync.dma_start(out=gc_t[:], in_=gc.rearrange("(g p t) -> p g t", g=G, t=PACK))
         w3_w_raw = keep.tile([P, G, 2 * N], U8, name="w3_w_raw", align_bytes=64)
         nc.sync.dma_start(out=w3_w_raw[:].bitcast(I32), in_=w3_words.rearrange("g p b -> p g b").bitcast(I32))
-        for q in range(4):
+        for q in range(QUADS):
             nc.sync.dma_start(
                 out=w3_s_raw[32 * q : 32 * q + 4].bitcast(I32),
                 in_=w3_scales[:, 4 * q : 4 * q + 4, :].rearrange("g r n -> r g n").bitcast(I32),
@@ -124,22 +125,20 @@ def tile_list_tide_sorted_growth_kernel(
         load_amp(2)
         load_wgo(1)
         load_amp(3)
-        halves = (slice(0, S // 2), slice(S // 2, S))
-        y = [keep.tile([P, PACK, S // 2], F32, name="y%d" % h) for h in range(2)]
-        for h, cols in enumerate(halves):
-            nc.sync.dma_start(out=y[h][:], in_=x0.rearrange("(p t) m -> p t m", t=PACK)[:, :, cols])
+        y_all = keep.tile([P, PACK, S], F32, name="y_all")
+        nc.sync.dma_start(out=y_all[:], in_=x0.rearrange("(p t) m -> p t m", t=PACK))
 
         v_w = {}
         v_s = {}
         for c in range(S // GATHER):
-            offsets = idx[:, c * GATHER // 16 : (c + 1) * GATHER // 16]
+            offsets = idx[:, c * GATHER // LIST_COL : (c + 1) * GATHER // LIST_COL]
             for a in range(G):
-                words = keep.tile([P, GATHER], U32, name="v_w%d_%d" % (c, a), align_bytes=64)
-                nc.vector.tensor_copy(out=words[:], in_=tab_w[a][:].indirect(offsets))
-                v_w[c, a] = words
-            planes = keep.tile([P, GATHER], U8, name="v_s%d" % c, align_bytes=64)
-            nc.vector.tensor_copy(out=planes[:], in_=tab_s[:].indirect(offsets))
-            v_s[c] = planes
+                picked_w = keep.tile([P, GATHER], U32, name="v_w%d_%d" % (c, a), align_bytes=64)
+                nc.vector.tensor_copy(out=picked_w[:], in_=tab_w[a][:].indirect(offsets))
+                v_w[c, a] = picked_w
+            picked_s = keep.tile([P, GATHER], U8, name="v_s%d" % c, align_bytes=64)
+            nc.vector.tensor_copy(out=picked_s[:], in_=tab_s[:].indirect(offsets))
+            v_s[c] = picked_s
 
         w2_w = keep.tile([P, G, N], U32, name="w2_w", align_bytes=64)
         w2_s = keep.tile([P, G, N], U8, name="w2_s", align_bytes=64)
@@ -150,10 +149,13 @@ def tile_list_tide_sorted_growth_kernel(
             for g in range(G):
                 w2_b = keep.tile([P, PACK, P, PACK], BF16, name="w2_b%d" % g, align_bytes=64)
                 nc.vector.tensor_copy(
-                    out=w2_b[:].rearrange("p t m j -> p m t j"), in_=w2_raw[g][:].rearrange("p j (m t) -> p m t j", t=PACK)
+                    out=w2_b[:].rearrange("p t m j -> p m t j"),
+                    in_=w2_raw[g][:].rearrange("p j (m t) -> p m t j", t=PACK),
                 )
                 nc.vector.quantize_mx(
-                    out=w2_w[:, g, :].bitcast(FP8X4), scales=w2_s[:, g, :], in_=w2_b[:].rearrange("p t m j -> p (t m j)")
+                    out=w2_w[:, g, :].bitcast(FP8X4),
+                    scales=w2_s[:, g, :],
+                    in_=w2_b[:].rearrange("p t m j -> p (t m j)"),
                 )
             nc.vector.tensor_copy(
                 out=w3_w[:].bitcast(U16).rearrange("p g (t m) -> p g t m", t=PACK),
@@ -170,14 +172,14 @@ def tile_list_tide_sorted_growth_kernel(
             c, lo = divmod(i * TOK, GATHER)
             banks = []
             for g in range(G):
-                a_t = psum.tile([P, 512], F32, name="a_t", bufs=2)
+                a_t = psum.tile([P, PASS], F32, name="a_t", bufs=2)
                 for a in range(G):
                     nc.tensor.matmul_mx(
                         out=a_t[:],
                         lhsT=v_w[c, a][:, lo : lo + TOK].bitcast(FP8X4),
                         lhsT_scale=v_s[c][4 * a :, lo : lo + TOK],
-                        rhs=w1_w[g][:, a, :].bitcast(FP8X4),
-                        rhs_scale=w1_s[4 * a :, 512 * g : 512 * (g + 1)],
+                        rhs=w1_w[a][:, PASS * g : PASS * (g + 1)].bitcast(FP8X4),
+                        rhs_scale=w1_s[4 * a :, PASS * g : PASS * (g + 1)],
                         start=(a == 0),
                         stop=(a == G - 1),
                     )
@@ -233,13 +235,13 @@ def tile_list_tide_sorted_growth_kernel(
             return sine, cosine, folded
 
         def weigh(i, sine, cosine):
-            quarter, lo = divmod(i * TOK, AMP_COLS)
+            part, lo = divmod(i * TOK, AMP_COLS)
             h_b = ring.tile([P, 2 * G, TOK, PACK], BF16, name="h_b", align_bytes=64)
             for g in range(G):
                 nc.vector.tensor_tensor(
-                    out=h_b[:, g].rearrange("p (c i) t -> p c t i", i=4),
-                    in0=sine[:, g].rearrange("p t (c i) -> p c t i", i=4),
-                    in1=amp_t[quarter, g][:, :, lo : lo + TOK].rearrange("p t (c i) -> p c t i", i=4),
+                    out=h_b[:, g].rearrange("p (c i) t -> p c t i", i=RUN),
+                    in0=sine[:, g].rearrange("p t (c i) -> p c t i", i=RUN),
+                    in1=amp_t[part, g][:, :, lo : lo + TOK].rearrange("p t (c i) -> p c t i", i=RUN),
                     op=ALU.mult,
                 )
             nc.vector.tensor_tensor(
@@ -259,13 +261,13 @@ def tile_list_tide_sorted_growth_kernel(
                 for o in range(2 * G):
                     g = o % G
                     if o < G:
-                        weights, scales = w2_w[:, g, cols].bitcast(FP8X4), w2_s[:, g, cols]
+                        w_w, w_s = w2_w[:, g, cols].bitcast(FP8X4), w2_s[:, g, cols]
                     else:
-                        weights, scales = w3_w[:, g, 2 * t * P : 2 * (t + 1) * P].bitcast(FP4X4), w3_s[:, g, cols]
+                        w_w, w_s = w3_w[:, g, 2 * t * P : 2 * (t + 1) * P].bitcast(FP4X4), w3_s[:, g, cols]
                     nc.tensor.matmul_mx(
                         out=d[:, t, :],
-                        lhsT=weights,
-                        lhsT_scale=scales,
+                        lhsT=w_w,
+                        lhsT_scale=w_s,
                         rhs=h_w[:, o * TOK : (o + 1) * TOK].bitcast(FP8X4),
                         rhs_scale=h_s[:, o * TOK : (o + 1) * TOK],
                         start=(o == 0),
@@ -278,12 +280,12 @@ def tile_list_tide_sorted_growth_kernel(
             nc.scalar.copy(out=d_sb, in_=d[:])
             return d_sb
 
-        def place(i, d_sb):
-            half, lo = divmod(i * TOK, WGO_COLS)
-            offsets = idx2[:, i * TOK // 16 : (i + 1) * TOK // 16]
-            for t in range(PACK):
+        def place(i, d_sb, rows):
+            part, lo = divmod(i * TOK, WGO_COLS)
+            offsets = idx2[:, i * TOK // LIST_COL : (i + 1) * TOK // LIST_COL]
+            for t in rows:
                 nc.vector.tensor_tensor(
-                    out=page[t][:].indirect(offsets), in0=d_sb[:, t, :], in1=wgo_t[half][:, t, lo : lo + TOK],
+                    out=page[t][:].indirect(offsets), in0=d_sb[:, t, :], in1=wgo_t[part][:, t, lo : lo + TOK],
                     op=ALU.mult,
                 )
 
@@ -306,35 +308,42 @@ def tile_list_tide_sorted_growth_kernel(
             if i == 0:
                 deal_weights()
             if i >= LAG:
-                place(i - LAG, d_sb)
+                place(i - LAG, d_sb, range(PACK))
         sums[TILES - 1] = growth(*codes[TILES - 1])
-        for r, i in enumerate(range(TILES - LAG, TILES)):
-            place(i, evacuate(sums[i], spent[:, r * PACK * TOK : (r + 1) * PACK * TOK]))
+        place(TILES - 2, evacuate(sums[TILES - 2], spent[:, : PACK * TOK]), range(PACK))
+        d_sb = evacuate(sums[TILES - 1], spent[:, PACK * TOK :])
 
+        y_rows = out_0.rearrange("(p t) m -> t p m", t=PACK)
+
+        def finish(t, cols):
+            y_t = y_all[:, t, :][:, cols]
+            nc.vector.tensor_tensor(out=y_t, in0=page[t][:, cols], in1=y_t, op=ALU.mult)
+            nc.sync.dma_start(out=y_rows[t][:, cols], in_=y_t)
+
+        for t in range(PACK):
+            place(TILES - 1, d_sb, (t,))
+            if t >= 1:
+                finish(t - 1, slice(0, S))
+
+        halves = (slice(0, S // 2), slice(S // 2, S))
         y_w = keep.tile([P, S], U32, name="y_w", align_bytes=64)
         y_s = keep.tile([P, S], U8, name="y_s", align_bytes=64)
         y_b = [keep.tile([P, S // 2, PACK], BF16, name="y_b%d" % h, align_bytes=64) for h in range(2)]
-        for h, cols in enumerate(halves):
-            for t in range(PACK):
-                nc.vector.tensor_tensor(out=y[h][:, t, :], in0=page[t][:, cols], in1=y[h][:, t, :], op=ALU.mult)
-            nc.sync.dma_start(
-                out=out_0.rearrange("(p t) m -> p t m", t=PACK)[:, :, cols], in_=y[h][:]
+        for cols in halves:
+            finish(PACK - 1, cols)
+        for y_half, cols, copy in zip(y_b, halves, (nc.scalar.copy, nc.vector.tensor_copy)):
+            copy(
+                out=y_half[:].rearrange("p (c i) t -> p c t i", i=RUN),
+                in_=y_all[:, :, cols].rearrange("p t (c i) -> p c t i", i=RUN),
             )
-            dst = y_b[h][:].rearrange("p (c i) t -> p c t i", i=4)
-            src = y[h][:].rearrange("p t (c i) -> p c t i", i=4)
-            if h == 0:
-                nc.scalar.copy(out=dst, in_=src)
-            else:
-                nc.vector.tensor_copy(out=dst, in_=src)
-        for h in (1, 0):
-            cols = halves[h]
+        for y_half, cols in reversed(list(zip(y_b, halves))):
             nc.vector.quantize_mx(
-                out=y_w[:, cols].bitcast(FP8X4), scales=y_s[:, cols], in_=y_b[h][:].rearrange("p c t -> p (c t)")
+                out=y_w[:, cols].bitcast(FP8X4), scales=y_s[:, cols], in_=y_half[:].rearrange("p c t -> p (c t)")
             )
             nc.sync.dma_start(
                 out=out_1[0][:, cols, :].rearrange("p c i -> p (c i)").bitcast(I32), in_=y_w[:, cols].bitcast(I32)
             )
-        for q in range(4):
+        for q in range(QUADS):
             nc.scalar.dma_start(
                 out=out_2[0][4 * q : 4 * q + 4, :].bitcast(I32), in_=y_s[32 * q : 32 * q + 4, :].bitcast(I32)
             )

@@ -220,10 +220,9 @@ def tile_list_tide_sorted_growth_kernel(
 
         def waves(banks):
             sine = ring.tile([P, G, PACK, TOK], F32, name="sine")
-            cosine = ring.tile([P, G, TOK, PACK], F32, name="cosine")
+            cosine = ring.tile([P, G, TOK, PACK], F32, name="cosine", bufs=3, align_bytes=64)
             folded = ring.tile([P, G, TOK * PACK], F32, name="folded")
             for g in range(G):
-                nc.scalar.activation(out=sine[:, g], in_=banks[g][:], func=ACT.Sin, scale=2.0 * math.pi)
                 nc.scalar.activation(
                     out=folded[:, g].rearrange("p (j t) -> p j t", t=PACK),
                     in_=banks[g][:].rearrange("p t j -> p j t"), func=ACT.Abs,
@@ -232,27 +231,37 @@ def tile_list_tide_sorted_growth_kernel(
                 out=cosine[:].rearrange("p g j t -> p (g j t)"), in_=folded[:].rearrange("p g e -> p (g e)"),
                 func=ACT.Sin, scale=-2.0 * math.pi, bias=math.pi / 2.0,
             )
-            return sine, cosine, folded
-
-        def weigh(i, sine, cosine):
-            part, lo = divmod(i * TOK, AMP_COLS)
-            h_b = ring.tile([P, 2 * G, TOK, PACK], BF16, name="h_b", align_bytes=64)
             for g in range(G):
+                nc.scalar.activation(out=sine[:, g], in_=banks[g][:], func=ACT.Sin, scale=2.0 * math.pi)
+            return sine, cosine
+
+        def rounded(cosine):
+            return cosine[:, 0].rearrange("p j t -> p (j t)").bitcast(BF16).rearrange(
+                "p (g j t) -> p g j t", g=G, t=PACK
+            )
+
+        def weigh_sine(i, sine, h_b):
+            part, lo = divmod(i * TOK, AMP_COLS)
+            for g in reversed(range(G)):
                 nc.vector.tensor_tensor(
                     out=h_b[:, g].rearrange("p (c i) t -> p c t i", i=RUN),
                     in0=sine[:, g].rearrange("p t (c i) -> p c t i", i=RUN),
                     in1=amp_t[part, g][:, :, lo : lo + TOK].rearrange("p t (c i) -> p c t i", i=RUN),
                     op=ALU.mult,
                 )
-            nc.vector.tensor_tensor(
-                out=h_b[:, G:], in0=cosine[:], in1=gc_t[:].unsqueeze(2).to_broadcast([P, G, TOK, PACK]), op=ALU.mult
+
+        def weigh_cosine(i, cosine, h_b):
+            engine = nc.gpsimd if i >= LAG else nc.vector
+            engine.tensor_tensor(
+                out=h_b, in0=cosine[:], in1=gc_t[:].unsqueeze(2).to_broadcast([P, G, TOK, PACK]), op=ALU.mult
             )
-            h_w = ring.tile([P, 2 * G * TOK], U32, name="h_w", align_bytes=64)
-            h_s = ring.tile([P, 2 * G * TOK], U8, name="h_s", align_bytes=64)
+
+        def quantise(h_w, h_s, o, h_b):
+            cols = slice(o * G * TOK, (o + 1) * G * TOK)
             nc.vector.quantize_mx(
-                out=h_w[:].bitcast(FP8X4), scales=h_s[:], in_=h_b[:].rearrange("p o j t -> p (o j t)")
+                out=h_w[:, cols].bitcast(FP8X4), scales=h_s[:, cols],
+                in_=h_b.rearrange("p g j t -> p (g j t)"),
             )
-            return (h_w, h_s), h_b[:].rearrange("p o j t -> p (o j t)").bitcast(F32)
 
         def growth(h_w, h_s):
             d = psum.tile([P, PACK, TOK], F32, name="d", bufs=2)
@@ -275,23 +284,21 @@ def tile_list_tide_sorted_growth_kernel(
                     )
             return d
 
-        def evacuate(d, scratch):
-            d_sb = scratch.rearrange("p (t j) -> p t j", t=PACK)
-            nc.scalar.copy(out=d_sb, in_=d[:])
-            return d_sb
+        def weigh_growth(i, d, scratch):
+            part, lo = divmod(i * TOK, WGO_COLS)
+            nc.vector.tensor_tensor(out=scratch, in0=d[:], in1=wgo_t[part][:, :, lo : lo + TOK], op=ALU.mult)
+            return scratch
 
         def place(i, d_sb, rows):
-            part, lo = divmod(i * TOK, WGO_COLS)
             offsets = idx2[:, i * TOK // LIST_COL : (i + 1) * TOK // LIST_COL]
             for t in rows:
-                nc.vector.tensor_tensor(
-                    out=page[t][:].indirect(offsets), in0=d_sb[:, t, :], in1=wgo_t[part][:, t, lo : lo + TOK],
-                    op=ALU.mult,
-                )
+                nc.vector.tensor_copy(out=page[t][:].indirect(offsets), in_=d_sb[:, t, :])
 
         turns = {i: to_turns(i, angles(i)) for i in range(2)}
         fracs = {0: reduce_turns(*turns[0])}
         codes, sums = {}, {}
+        first_h_b = keep.tile([P, G, TOK, PACK], BF16, name="first_h_b", align_bytes=64)
+        h_b = first_h_b[:]
         for i in range(TILES):
             if i + 2 < TILES:
                 a_banks = angles(i + 2)
@@ -299,19 +306,27 @@ def tile_list_tide_sorted_growth_kernel(
                 fracs[i + 1] = reduce_turns(*turns[i + 1])
             if i >= 1:
                 sums[i - 1] = growth(*codes[i - 1])
-            sine, cosine, folded = waves(fracs[i])
-            if i >= LAG:
-                d_sb = evacuate(sums[i - LAG], folded[:, 0])
+            sine, cosine = waves(fracs[i])
             if i + 2 < TILES:
                 turns[i + 2] = to_turns(i + 2, a_banks)
-            codes[i], spent = weigh(i, sine, cosine)
-            if i == 0:
-                deal_weights()
+            h_w = ring.tile([P, 2 * G * TOK], U32, name="h_w", align_bytes=64)
+            h_s = ring.tile([P, 2 * G * TOK], U8, name="h_s", align_bytes=64)
+            codes[i] = (h_w, h_s)
+            weigh_sine(i, sine, h_b)
+            if i >= LAG:
+                d_sb = weigh_growth(i - LAG, sums[i - LAG], sine[:, G - 1])
+            quantise(h_w, h_s, 0, h_b)
+            weigh_cosine(i, cosine, h_b)
             if i >= LAG:
                 place(i - LAG, d_sb, range(PACK))
+            quantise(h_w, h_s, 1, h_b)
+            h_b = rounded(cosine)
+            if i == 0:
+                deal_weights()
         sums[TILES - 1] = growth(*codes[TILES - 1])
-        place(TILES - 2, evacuate(sums[TILES - 2], spent[:, : PACK * TOK]), range(PACK))
-        d_sb = evacuate(sums[TILES - 1], spent[:, PACK * TOK :])
+        spent = [cosine[:, g].rearrange("p j t -> p (j t)").rearrange("p (t j) -> p t j", t=PACK) for g in range(G)]
+        place(TILES - 2, weigh_growth(TILES - 2, sums[TILES - 2], spent[0]), range(PACK))
+        d_sb = weigh_growth(TILES - 1, sums[TILES - 1], spent[1])
 
         y_rows = out_0.rearrange("(p t) m -> t p m", t=PACK)
 

@@ -263,30 +263,32 @@ def tile_list_tide_sorted_growth_kernel(
                 in_=h_b.rearrange("p g j t -> p (g j t)"),
             )
 
-        def growth(h_w, h_s):
+        def growth(h_w, h_s, by_pass=False):
             d = psum.tile([P, PACK, TOK], F32, name="d", bufs=2)
-            for t in range(PACK):
+            steps = [(t, o) for t in range(PACK) for o in range(2 * G)]
+            if by_pass:
+                steps = [(t, o) for o in range(2 * G) for t in range(PACK)]
+            for t, o in steps:
                 cols = slice(t * P, (t + 1) * P)
-                for o in range(2 * G):
-                    g = o % G
-                    if o < G:
-                        w_w, w_s = w2_w[:, g, cols].bitcast(FP8X4), w2_s[:, g, cols]
-                    else:
-                        w_w, w_s = w3_w[:, g, 2 * t * P : 2 * (t + 1) * P].bitcast(FP4X4), w3_s[:, g, cols]
-                    nc.tensor.matmul_mx(
-                        out=d[:, t, :],
-                        lhsT=w_w,
-                        lhsT_scale=w_s,
-                        rhs=h_w[:, o * TOK : (o + 1) * TOK].bitcast(FP8X4),
-                        rhs_scale=h_s[:, o * TOK : (o + 1) * TOK],
-                        start=(o == 0),
-                        stop=(o == 2 * G - 1),
-                    )
+                g = o % G
+                if o < G:
+                    w_w, w_s = w2_w[:, g, cols].bitcast(FP8X4), w2_s[:, g, cols]
+                else:
+                    w_w, w_s = w3_w[:, g, 2 * t * P : 2 * (t + 1) * P].bitcast(FP4X4), w3_s[:, g, cols]
+                nc.tensor.matmul_mx(
+                    out=d[:, t, :],
+                    lhsT=w_w,
+                    lhsT_scale=w_s,
+                    rhs=h_w[:, o * TOK : (o + 1) * TOK].bitcast(FP8X4),
+                    rhs_scale=h_s[:, o * TOK : (o + 1) * TOK],
+                    start=(t, o) == steps[0] if by_pass else o == 0,
+                    stop=(t, o) == steps[-1] if by_pass else o == 2 * G - 1,
+                )
             return d
 
-        def weigh_growth(i, d, scratch):
+        def weigh_growth(i, d, scratch, rows=slice(0, PACK)):
             part, lo = divmod(i * TOK, WGO_COLS)
-            nc.vector.tensor_tensor(out=scratch, in0=d[:], in1=wgo_t[part][:, :, lo : lo + TOK], op=ALU.mult)
+            nc.vector.tensor_tensor(out=scratch, in0=d[:, rows], in1=wgo_t[part][:, rows, lo : lo + TOK], op=ALU.mult)
             return scratch
 
         def place(i, d_sb, rows):
@@ -323,29 +325,36 @@ def tile_list_tide_sorted_growth_kernel(
             h_b = rounded(cosine)
             if i == 0:
                 deal_weights()
-        sums[TILES - 1] = growth(*codes[TILES - 1])
+        sums[TILES - 1] = growth(*codes[TILES - 1], by_pass=True)
         spent = [cosine[:, g].rearrange("p j t -> p (j t)").rearrange("p (t j) -> p t j", t=PACK) for g in range(G)]
-        place(TILES - 2, weigh_growth(TILES - 2, sums[TILES - 2], spent[0]), range(PACK))
+        early = weigh_growth(TILES - 2, sums[TILES - 2], spent[0][:, :1], slice(0, 1))
+        place(TILES - 2, early, range(1))
         d_sb = weigh_growth(TILES - 1, sums[TILES - 1], spent[1])
+        last_wgo = wgo_t[S // WGO_COLS - 1][:, :, WGO_COLS - TOK :]
+        weigh_growth(TILES - 2, sums[TILES - 2], last_wgo[:, 1:], slice(1, PACK))
 
         y_rows = out_0.rearrange("(p t) m -> t p m", t=PACK)
 
-        def finish(t, cols):
+        def finish(engine, t, cols):
             y_t = y_all[:, t, :][:, cols]
-            nc.vector.tensor_tensor(out=y_t, in0=page[t][:, cols], in1=y_t, op=ALU.mult)
+            engine.tensor_tensor(out=y_t, in0=page[t][:, cols], in1=y_t, op=ALU.mult)
             nc.sync.dma_start(out=y_rows[t][:, cols], in_=y_t)
 
-        for t in range(PACK):
-            place(TILES - 1, d_sb, (t,))
-            if t >= 1:
-                finish(t - 1, slice(0, S))
+        place(TILES - 1, d_sb, (0,))
+        finish(nc.gpsimd, 0, slice(0, S))
+        place(TILES - 2, last_wgo, (1, 2))
+        place(TILES - 1, d_sb, (1,))
+        finish(nc.gpsimd, 1, slice(0, S))
+        place(TILES - 2, last_wgo, (3,))
+        place(TILES - 1, d_sb, (2, 3))
+        finish(nc.vector, 2, slice(0, S))
 
         halves = (slice(0, S // 2), slice(S // 2, S))
         y_w = keep.tile([P, S], U32, name="y_w", align_bytes=64)
         y_s = keep.tile([P, S], U8, name="y_s", align_bytes=64)
         y_b = [keep.tile([P, S // 2, PACK], BF16, name="y_b%d" % h, align_bytes=64) for h in range(2)]
         for cols in halves:
-            finish(PACK - 1, cols)
+            finish(nc.vector, PACK - 1, cols)
         for y_half, cols, copy in zip(y_b, halves, (nc.scalar.copy, nc.vector.tensor_copy)):
             copy(
                 out=y_half[:].rearrange("p (c i) t -> p c t i", i=RUN),

@@ -223,6 +223,8 @@ def tile_list_tide_sorted_growth_kernel(
             cosine = ring.tile([P, G, TOK, PACK], F32, name="cosine", bufs=3, align_bytes=64)
             folded = ring.tile([P, G, TOK * PACK], F32, name="folded")
             for g in range(G):
+                nc.scalar.activation(out=sine[:, g], in_=banks[g][:], func=ACT.Sin, scale=2.0 * math.pi)
+            for g in range(G):
                 nc.scalar.activation(
                     out=folded[:, g].rearrange("p (j t) -> p j t", t=PACK),
                     in_=banks[g][:].rearrange("p t j -> p j t"), func=ACT.Abs,
@@ -231,8 +233,6 @@ def tile_list_tide_sorted_growth_kernel(
                 out=cosine[:].rearrange("p g j t -> p (g j t)"), in_=folded[:].rearrange("p g e -> p (g e)"),
                 func=ACT.Sin, scale=-2.0 * math.pi, bias=math.pi / 2.0,
             )
-            for g in range(G):
-                nc.scalar.activation(out=sine[:, g], in_=banks[g][:], func=ACT.Sin, scale=2.0 * math.pi)
             return sine, cosine
 
         def rounded(cosine):

@@ -168,34 +168,30 @@ def tile_list_tide_sorted_growth_kernel(
 
         page = [keep.tile([P, S], F32, name="page%d" % t) for t in range(PACK)]
 
-        def angles(i):
+        def angles(i, g):
             c, lo = divmod(i * TOK, GATHER)
-            banks = []
-            for g in range(G):
-                a_t = psum.tile([P, PASS], F32, name="a_t", bufs=2)
-                for a in range(G):
-                    nc.tensor.matmul_mx(
-                        out=a_t[:],
-                        lhsT=v_w[c, a][:, lo : lo + TOK].bitcast(FP8X4),
-                        lhsT_scale=v_s[c][4 * a :, lo : lo + TOK],
-                        rhs=w1_w[a][:, PASS * g : PASS * (g + 1)].bitcast(FP8X4),
-                        rhs_scale=w1_s[4 * a :, PASS * g : PASS * (g + 1)],
-                        start=(a == 0),
-                        stop=(a == G - 1),
-                    )
-                banks.append(a_t)
-            return banks
-
-        def to_turns(i, banks):
-            turns = ring.tile([P, G, PACK, P], F32, name="turns", bufs=3)
-            for g in range(G):
-                nc.scalar.activation(
-                    out=turns[:, g], in_=banks[g][:].rearrange("j (p t) -> j t p", t=PACK), func=ACT.Copy,
-                    scale=1.0 / (2.0 * math.pi),
+            a_t = psum.tile([P, PASS], F32, name="a_t", bufs=2)
+            for a in range(G):
+                nc.tensor.matmul_mx(
+                    out=a_t[:],
+                    lhsT=v_w[c, a][:, lo : lo + TOK].bitcast(FP8X4),
+                    lhsT_scale=v_s[c][4 * a :, lo : lo + TOK],
+                    rhs=w1_w[a][:, PASS * g : PASS * (g + 1)].bitcast(FP8X4),
+                    rhs_scale=w1_s[4 * a :, PASS * g : PASS * (g + 1)],
+                    start=(a == 0),
+                    stop=(a == G - 1),
                 )
-            whole = ring.tile([P, G, PACK, P], U32, name="whole", bufs=3)
-            src = turns[:].rearrange("j g t p -> j (g t p)")
-            dst = whole[:].rearrange("j g t p -> j (g t p)")
+            return a_t
+
+        def to_turns(i, bank):
+            turns = ring.tile([P, PACK, P], F32, name="turns", bufs=6)
+            nc.scalar.activation(
+                out=turns[:], in_=bank[:].rearrange("j (p t) -> j t p", t=PACK), func=ACT.Copy,
+                scale=1.0 / (2.0 * math.pi),
+            )
+            whole = ring.tile([P, PACK, P], U32, name="whole", bufs=6)
+            src = turns[:].rearrange("j t p -> j (t p)")
+            dst = whole[:].rearrange("j t p -> j (t p)")
             if i in ROUNDED_ON_VECTOR:
                 nc.vector.tensor_scalar(
                     out=dst.bitcast(I32), in0=src, scalar1=-TURN_STEP, scalar2=TURN_BITS, op0=ALU.mult, op1=ALU.add
@@ -205,18 +201,15 @@ def tile_list_tide_sorted_growth_kernel(
             return turns, whole
 
         def reduce_turns(turns, whole):
-            banks = []
-            for g in range(G):
-                frac = psum.tile([P, PACK, TOK], F32, name="frac", bufs=4)
-                for t in range(PACK):
-                    terms = (minus_base[:], whole[:, g, t, :].bitcast(F32), turns[:, g, t, :])
-                    for s, term in enumerate(terms):
-                        nc.tensor.matmul(
-                            out=frac[:, t, :], lhsT=term, rhs=ident[:], is_transpose=True,
-                            start=(s == 0), stop=(s == len(terms) - 1),
-                        )
-                banks.append(frac)
-            return banks
+            frac = psum.tile([P, PACK, TOK], F32, name="frac", bufs=3)
+            for t in range(PACK):
+                terms = (minus_base[:], whole[:, t, :].bitcast(F32), turns[:, t, :])
+                for s, term in enumerate(terms):
+                    nc.tensor.matmul(
+                        out=frac[:, t, :], lhsT=term, rhs=ident[:], is_transpose=True,
+                        start=(s == 0), stop=(s == len(terms) - 1),
+                    )
+            return frac
 
         def waves(banks):
             sine = ring.tile([P, G, PACK, TOK], F32, name="sine")
@@ -263,28 +256,24 @@ def tile_list_tide_sorted_growth_kernel(
                 in_=h_b.rearrange("p g j t -> p (g j t)"),
             )
 
-        def growth(h_w, h_s, by_pass=False):
-            d = psum.tile([P, PACK, TOK], F32, name="d", bufs=2)
-            steps = [(t, o) for t in range(PACK) for o in range(2 * G)]
-            if by_pass:
-                steps = [(t, o) for o in range(2 * G) for t in range(PACK)]
-            for t, o in steps:
-                cols = slice(t * P, (t + 1) * P)
-                g = o % G
-                if o < G:
-                    w_w, w_s = w2_w[:, g, cols].bitcast(FP8X4), w2_s[:, g, cols]
-                else:
-                    w_w, w_s = w3_w[:, g, 2 * t * P : 2 * (t + 1) * P].bitcast(FP4X4), w3_s[:, g, cols]
-                nc.tensor.matmul_mx(
-                    out=d[:, t, :],
-                    lhsT=w_w,
-                    lhsT_scale=w_s,
-                    rhs=h_w[:, o * TOK : (o + 1) * TOK].bitcast(FP8X4),
-                    rhs_scale=h_s[:, o * TOK : (o + 1) * TOK],
-                    start=(t, o) == steps[0] if by_pass else o == 0,
-                    stop=(t, o) == steps[-1] if by_pass else o == 2 * G - 1,
-                )
-            return d
+        def growth(d, o, h_w, h_s):
+            for g in range(G):
+                h_cols = slice((o * G + g) * TOK, (o * G + g + 1) * TOK)
+                for t in range(PACK):
+                    cols = slice(t * P, (t + 1) * P)
+                    if o == 0:
+                        w_w, w_s = w2_w[:, g, cols].bitcast(FP8X4), w2_s[:, g, cols]
+                    else:
+                        w_w, w_s = w3_w[:, g, 2 * t * P : 2 * (t + 1) * P].bitcast(FP4X4), w3_s[:, g, cols]
+                    nc.tensor.matmul_mx(
+                        out=d[:, t, :],
+                        lhsT=w_w,
+                        lhsT_scale=w_s,
+                        rhs=h_w[:, h_cols].bitcast(FP8X4),
+                        rhs_scale=h_s[:, h_cols],
+                        start=(o, g, t) == (0, 0, 0),
+                        stop=(o, g, t) == (1, G - 1, PACK - 1),
+                    )
 
         def weigh_growth(i, d, scratch, rows=slice(0, PACK)):
             part, lo = divmod(i * TOK, WGO_COLS)
@@ -296,21 +285,28 @@ def tile_list_tide_sorted_growth_kernel(
             for t in rows:
                 nc.vector.tensor_copy(out=page[t][:].indirect(offsets), in_=d_sb[:, t, :])
 
-        turns = {i: to_turns(i, angles(i)) for i in range(2)}
-        fracs = {0: reduce_turns(*turns[0])}
-        codes, sums = {}, {}
+        a_banks, turns, fracs, codes, sums = {}, {}, {}, {}, {}
+        for i in range(2):
+            for g in range(G):
+                a_banks[i, g] = angles(i, g)
+            for g in range(G):
+                turns[i, g] = to_turns(i, a_banks[i, g])
+        for g in range(G):
+            fracs[0, g] = reduce_turns(*turns[0, g])
+        a_banks[2, 0] = angles(2, 0)
+        fracs[1, 0] = reduce_turns(*turns[1, 0])
+        a_banks[2, 1] = angles(2, 1)
         first_h_b = keep.tile([P, G, TOK, PACK], BF16, name="first_h_b", align_bytes=64)
         h_b = first_h_b[:]
         for i in range(TILES):
-            if i + 2 < TILES:
-                a_banks = angles(i + 2)
-            if i + 1 < TILES:
-                fracs[i + 1] = reduce_turns(*turns[i + 1])
             if i >= 1:
-                sums[i - 1] = growth(*codes[i - 1])
-            sine, cosine = waves(fracs[i])
+                growth(sums[i - 1], 1, *codes[i - 1])
+            if i + 1 < TILES:
+                fracs[i + 1, 1] = reduce_turns(*turns[i + 1, 1])
+            sine, cosine = waves([fracs[i, g] for g in range(G)])
             if i + 2 < TILES:
-                turns[i + 2] = to_turns(i + 2, a_banks)
+                for g in range(G):
+                    turns[i + 2, g] = to_turns(i + 2, a_banks[i + 2, g])
             h_w = ring.tile([P, 2 * G * TOK], U32, name="h_w", align_bytes=64)
             h_s = ring.tile([P, 2 * G * TOK], U8, name="h_s", align_bytes=64)
             codes[i] = (h_w, h_s)
@@ -325,7 +321,15 @@ def tile_list_tide_sorted_growth_kernel(
             h_b = rounded(cosine)
             if i == 0:
                 deal_weights()
-        sums[TILES - 1] = growth(*codes[TILES - 1], by_pass=True)
+            sums[i] = psum.tile([P, PACK, TOK], F32, name="d", bufs=2)
+            growth(sums[i], 0, *codes[i])
+            if i + 3 < TILES:
+                a_banks[i + 3, 0] = angles(i + 3, 0)
+            if i + 2 < TILES:
+                fracs[i + 2, 0] = reduce_turns(*turns[i + 2, 0])
+            if i + 3 < TILES:
+                a_banks[i + 3, 1] = angles(i + 3, 1)
+        growth(sums[TILES - 1], 1, *codes[TILES - 1])
         spent = [cosine[:, g].rearrange("p j t -> p (j t)").rearrange("p (t j) -> p t j", t=PACK) for g in range(G)]
         early = weigh_growth(TILES - 2, sums[TILES - 2], spent[0][:, :1], slice(0, 1))
         place(TILES - 2, early, range(1))

@@ -27,6 +27,7 @@ TOK = 128
 TILES = S // TOK
 LIST_COL = 16
 RUN = 4
+PAIR = 2
 GATHER = 256
 AMP_COLS = 256
 WGO_COLS = 512
@@ -183,12 +184,15 @@ def tile_list_tide_sorted_growth_kernel(
                 )
             return a_t
 
-        def to_turns(i, bank):
+        def to_turns(bank):
             turns = ring.tile([P, PACK, P], F32, name="turns", bufs=6)
             nc.scalar.activation(
                 out=turns[:], in_=bank[:].rearrange("j (p t) -> j t p", t=PACK), func=ACT.Copy,
                 scale=1.0 / (2.0 * math.pi),
             )
+            return turns
+
+        def to_whole(i, turns):
             whole = ring.tile([P, PACK, P], U32, name="whole", bufs=6)
             src = turns[:].rearrange("j t p -> j (t p)")
             dst = whole[:].rearrange("j t p -> j (t p)")
@@ -216,16 +220,20 @@ def tile_list_tide_sorted_growth_kernel(
             cosine = ring.tile([P, G, TOK, PACK], F32, name="cosine", bufs=3, align_bytes=64)
             folded = ring.tile([P, G, TOK * PACK], F32, name="folded")
             for g in range(G):
-                nc.scalar.activation(out=sine[:, g], in_=banks[g][:], func=ACT.Sin, scale=2.0 * math.pi)
+                nc.scalar.activation(
+                    out=sine[:, g].rearrange("p t j -> p (t j)").rearrange("p (c t i) -> p c t i", t=PACK, i=PAIR),
+                    in_=banks[g][:].rearrange("p t (c i) -> p c t i", i=PAIR), func=ACT.Sin, scale=2.0 * math.pi,
+                )
             for g in range(G):
                 nc.scalar.activation(
                     out=folded[:, g].rearrange("p (j t) -> p j t", t=PACK),
                     in_=banks[g][:].rearrange("p t j -> p j t"), func=ACT.Abs,
                 )
-            nc.scalar.activation(
-                out=cosine[:].rearrange("p g j t -> p (g j t)"), in_=folded[:].rearrange("p g e -> p (g e)"),
-                func=ACT.Sin, scale=-2.0 * math.pi, bias=math.pi / 2.0,
-            )
+            for g in range(G):
+                nc.scalar.activation(
+                    out=cosine[:, g].rearrange("p j t -> p (j t)"), in_=folded[:, g],
+                    func=ACT.Sin, scale=-2.0 * math.pi, bias=math.pi / 2.0,
+                )
             return sine, cosine
 
         def rounded(cosine):
@@ -237,9 +245,9 @@ def tile_list_tide_sorted_growth_kernel(
             part, lo = divmod(i * TOK, AMP_COLS)
             for g in reversed(range(G)):
                 nc.vector.tensor_tensor(
-                    out=h_b[:, g].rearrange("p (c i) t -> p c t i", i=RUN),
-                    in0=sine[:, g].rearrange("p t (c i) -> p c t i", i=RUN),
-                    in1=amp_t[part, g][:, :, lo : lo + TOK].rearrange("p t (c i) -> p c t i", i=RUN),
+                    out=h_b[:, g].rearrange("p (c i) t -> p c t i", i=PAIR),
+                    in0=sine[:, g].rearrange("p t j -> p (t j)").rearrange("p (c t i) -> p c t i", t=PACK, i=PAIR),
+                    in1=amp_t[part, g][:, :, lo : lo + TOK].rearrange("p t (c i) -> p c t i", i=PAIR),
                     op=ALU.mult,
                 )
 
@@ -289,8 +297,9 @@ def tile_list_tide_sorted_growth_kernel(
         for i in range(2):
             for g in range(G):
                 a_banks[i, g] = angles(i, g)
+            both = [to_turns(a_banks[i, g]) for g in range(G)]
             for g in range(G):
-                turns[i, g] = to_turns(i, a_banks[i, g])
+                turns[i, g] = to_whole(i, both[g])
         for g in range(G):
             fracs[0, g] = reduce_turns(*turns[0, g])
         a_banks[2, 0] = angles(2, 0)
@@ -305,8 +314,9 @@ def tile_list_tide_sorted_growth_kernel(
                 fracs[i + 1, 1] = reduce_turns(*turns[i + 1, 1])
             sine, cosine = waves([fracs[i, g] for g in range(G)])
             if i + 2 < TILES:
+                both = [to_turns(a_banks[i + 2, g]) for g in range(G)]
                 for g in range(G):
-                    turns[i + 2, g] = to_turns(i + 2, a_banks[i + 2, g])
+                    turns[i + 2, g] = to_whole(i + 2, both[g])
             h_w = ring.tile([P, 2 * G * TOK], U32, name="h_w", align_bytes=64)
             h_s = ring.tile([P, 2 * G * TOK], U8, name="h_s", align_bytes=64)
             codes[i] = (h_w, h_s)

@@ -30,9 +30,9 @@ RUN = 4
 PAIR = 2
 GATHER = 256
 AMP_COLS = 256
-WGO_COLS = 512
 LAG = 2
-ROUNDED_ON_VECTOR = (1, 2, 3)
+ROUNDED_ON_VECTOR = (2, 3)
+WGO_PARTS = ((0, 512), (512, 1024))
 
 TURN_BASE = 98304.0
 TURN_BITS = 1203765248.0
@@ -55,7 +55,7 @@ def tile_list_tide_sorted_growth_kernel(
 
         tab_w = [keep.tile([P, T], U32, name="tab_w%d" % a, align_bytes=64) for a in range(G)]
         tab_s = keep.tile([P, T], U8, name="tab_s", align_bytes=64)
-        w1_w = [keep.tile([P, H], U32, name="w1_w%d" % a, align_bytes=64) for a in range(G)]
+        w1_w = [keep.tile([P, G, PASS], U32, name="w1_w%d" % g, align_bytes=64) for g in range(G)]
         w1_s = keep.tile([P, H], U8, name="w1_s", align_bytes=64)
         w3_s_raw = keep.tile([P, G, N], U8, name="w3_s_raw", align_bytes=64)
         ident = keep.tile([P, P], F32, name="ident")
@@ -84,8 +84,9 @@ def tile_list_tide_sorted_growth_kernel(
         load_words(tab_w[1][:], tab_words[1])
         for q in range(QUADS // 2, QUADS):
             load_scales(w1_s, w1_scales, q)
-        for a in range(G):
-            load_words(w1_w[a][:], w1_words[a])
+        w1_cols = w1_words.rearrange("a p c i -> p a (c i)").bitcast(I32)
+        for g in range(G):
+            nc.sync.dma_start(out=w1_w[g][:].bitcast(I32), in_=w1_cols[:, :, PASS * g : PASS * (g + 1)])
 
         amp_rows = amp.rearrange("(g p t) j -> g p t j", g=G, t=PACK)
         amp_t = {}
@@ -99,18 +100,18 @@ def tile_list_tide_sorted_growth_kernel(
         wgo_rows = wgo.rearrange("(q t) j -> q t j", t=PACK)
         wgo_t = {}
 
-        def load_wgo(part):
-            piece = keep.tile([P, PACK, WGO_COLS], F32, name="wgo%d" % part)
+        def load_wgo(lo, hi):
+            piece = keep.tile([P, PACK, hi - lo], F32, name="wgo%d" % lo)
             for q in range(QUADS):
-                nc.sync.dma_start(
-                    out=piece[32 * q : 32 * q + 32], in_=wgo_rows[:, :, part * WGO_COLS : (part + 1) * WGO_COLS]
-                )
-            wgo_t[part] = piece
+                nc.sync.dma_start(out=piece[32 * q : 32 * q + 32], in_=wgo_rows[:, :, lo:hi])
+            for i in range(lo // TOK, hi // TOK):
+                wgo_t[i] = piece[:, :, i * TOK - lo : (i + 1) * TOK - lo]
 
-        load_amp(0)
-        w2_raw = [keep.tile([P, PACK, N], F32, name="w2_raw%d" % g) for g in range(G)]
+        w2_raw = [keep.tile([P, PACK, N], F32, name="w2_raw%d" % g, align_bytes=64) for g in range(G)]
+        w2_rows = w2.rearrange("(g p j) n -> g p j n", g=G, j=PACK)
         for g in range(G):
-            nc.sync.dma_start(out=w2_raw[g][:], in_=w2.rearrange("(g p j) n -> g p j n", g=G, j=PACK)[g])
+            nc.sync.dma_start(out=w2_raw[g][:], in_=w2_rows[g])
+        load_amp(0)
         gc_t = keep.tile([P, G, PACK], F32, name="gc_t")
         nc.sync.dma_start(out=gc_t[:], in_=gc.rearrange("(g p t) -> p g t", g=G, t=PACK))
         w3_w_raw = keep.tile([P, G, 2 * N], U8, name="w3_w_raw", align_bytes=64)
@@ -120,44 +121,54 @@ def tile_list_tide_sorted_growth_kernel(
                 out=w3_s_raw[32 * q : 32 * q + 4].bitcast(I32),
                 in_=w3_scales[:, 4 * q : 4 * q + 4, :].rearrange("g r n -> r g n").bitcast(I32),
             )
+        load_wgo(*WGO_PARTS[0])
         nc.sync.dma_start(idx2[:], offs2)
-        load_wgo(0)
         load_amp(1)
         load_amp(2)
-        load_wgo(1)
+        load_wgo(*WGO_PARTS[1])
         load_amp(3)
         y_all = keep.tile([P, PACK, S], F32, name="y_all")
         nc.sync.dma_start(out=y_all[:], in_=x0.rearrange("(p t) m -> p t m", t=PACK))
 
-        v_w = {}
-        v_s = {}
-        for c in range(S // GATHER):
-            offsets = idx[:, c * GATHER // LIST_COL : (c + 1) * GATHER // LIST_COL]
-            for a in range(G):
-                picked_w = keep.tile([P, GATHER], U32, name="v_w%d_%d" % (c, a), align_bytes=64)
-                nc.vector.tensor_copy(out=picked_w[:], in_=tab_w[a][:].indirect(offsets))
-                v_w[c, a] = picked_w
-            picked_s = keep.tile([P, GATHER], U8, name="v_s%d" % c, align_bytes=64)
-            nc.vector.tensor_copy(out=picked_s[:], in_=tab_s[:].indirect(offsets))
-            v_s[c] = picked_s
+        picked = {}
+
+        def look_up(key, window, dst, lo, hi, at=0):
+            offsets = idx[:, lo // LIST_COL : hi // LIST_COL]
+            nc.vector.tensor_copy(out=dst[:, at : at + hi - lo], in_=window[:].indirect(offsets))
+            for i in range(lo // TOK, hi // TOK):
+                picked[key, i] = dst[:, at + i * TOK - lo : at + (i + 1) * TOK - lo]
+
+        v_first = keep.tile([P, S], U32, name="v_first", align_bytes=64)
+        v_second = keep.tile([P, S // 2 + TOK], U32, name="v_second", align_bytes=64)
+        v_next = keep.tile([P, GATHER], U32, name="v_next", align_bytes=64)
+        v_s = keep.tile([P, S - GATHER + TOK], U8, name="v_s", align_bytes=64)
+        look_up(0, tab_w[0], v_first, 0, S)
+        look_up("s", tab_s, v_s, 0, GATHER, at=S - GATHER - TOK)
+        look_up(1, tab_w[1], v_second, 0, GATHER, at=S // 2 - TOK)
+        look_up(1, tab_w[1], v_next, GATHER, 2 * GATHER)
+
+        warm = keep.tile([P, 1], F32, name="warm")
+        nc.scalar.activation(out=warm[:], in_=ident[:, 0:1], func=ACT.Sin)
 
         w2_w = keep.tile([P, G, N], U32, name="w2_w", align_bytes=64)
         w2_s = keep.tile([P, G, N], U8, name="w2_s", align_bytes=64)
         w3_w = keep.tile([P, G, 2 * N], U8, name="w3_w", align_bytes=64)
         w3_s = keep.tile([P, G, N], U8, name="w3_s", align_bytes=64)
 
-        def deal_weights():
-            for g in range(G):
-                w2_b = keep.tile([P, PACK, P, PACK], BF16, name="w2_b%d" % g, align_bytes=64)
-                nc.vector.tensor_copy(
-                    out=w2_b[:].rearrange("p t m j -> p m t j"),
-                    in_=w2_raw[g][:].rearrange("p j (m t) -> p m t j", t=PACK),
-                )
-                nc.vector.quantize_mx(
-                    out=w2_w[:, g, :].bitcast(FP8X4),
-                    scales=w2_s[:, g, :],
-                    in_=w2_b[:].rearrange("p t m j -> p (t m j)"),
-                )
+        def deal_w2(g):
+            w2_b = keep.tile([P, PACK, P, PACK], BF16, name="w2_b%d" % g, align_bytes=64)
+            nc.vector.tensor_copy(
+                out=w2_b[:].rearrange("p t m j -> p m t j"),
+                in_=w2_raw[g][:].rearrange("p j (m t) -> p m t j", t=PACK),
+            )
+            nc.vector.quantize_mx(
+                out=w2_w[:, g, :].bitcast(FP8X4),
+                scales=w2_s[:, g, :],
+                in_=w2_b[:].rearrange("p t m j -> p (t m j)"),
+            )
+            return w2_b
+
+        def deal_w3():
             nc.vector.tensor_copy(
                 out=w3_w[:].bitcast(U16).rearrange("p g (t m) -> p g t m", t=PACK),
                 in_=w3_w_raw[:].bitcast(U16).rearrange("p g (m t) -> p g t m", t=PACK),
@@ -170,14 +181,13 @@ def tile_list_tide_sorted_growth_kernel(
         page = [keep.tile([P, S], F32, name="page%d" % t) for t in range(PACK)]
 
         def angles(i, g):
-            c, lo = divmod(i * TOK, GATHER)
             a_t = psum.tile([P, PASS], F32, name="a_t", bufs=2)
             for a in range(G):
                 nc.tensor.matmul_mx(
                     out=a_t[:],
-                    lhsT=v_w[c, a][:, lo : lo + TOK].bitcast(FP8X4),
-                    lhsT_scale=v_s[c][4 * a :, lo : lo + TOK],
-                    rhs=w1_w[a][:, PASS * g : PASS * (g + 1)].bitcast(FP8X4),
+                    lhsT=picked[a, i].bitcast(FP8X4),
+                    lhsT_scale=picked["s", i][4 * a :, :],
+                    rhs=w1_w[g][:, a, :].bitcast(FP8X4),
                     rhs_scale=w1_s[4 * a :, PASS * g : PASS * (g + 1)],
                     start=(a == 0),
                     stop=(a == G - 1),
@@ -236,8 +246,8 @@ def tile_list_tide_sorted_growth_kernel(
                 )
             return sine, cosine
 
-        def rounded(cosine):
-            return cosine[:, 0].rearrange("p j t -> p (j t)").bitcast(BF16).rearrange(
+        def rounded(cosine, half=0):
+            return cosine[:, half].rearrange("p j t -> p (j t)").bitcast(BF16).rearrange(
                 "p (g j t) -> p g j t", g=G, t=PACK
             )
 
@@ -284,8 +294,7 @@ def tile_list_tide_sorted_growth_kernel(
                     )
 
         def weigh_growth(i, d, scratch, rows=slice(0, PACK)):
-            part, lo = divmod(i * TOK, WGO_COLS)
-            nc.vector.tensor_tensor(out=scratch, in0=d[:, rows], in1=wgo_t[part][:, rows, lo : lo + TOK], op=ALU.mult)
+            nc.vector.tensor_tensor(out=scratch, in0=d[:, rows], in1=wgo_t[i][:, rows], op=ALU.mult)
             return scratch
 
         def place(i, d_sb, rows):
@@ -297,6 +306,9 @@ def tile_list_tide_sorted_growth_kernel(
         for i in range(2):
             for g in range(G):
                 a_banks[i, g] = angles(i, g)
+            if i == 0:
+                look_up("s", tab_s, v_s, GATHER, S)
+                look_up(1, tab_w[1], v_second, 2 * GATHER, S)
             both = [to_turns(a_banks[i, g]) for g in range(G)]
             for g in range(G):
                 turns[i, g] = to_whole(i, both[g])
@@ -305,8 +317,9 @@ def tile_list_tide_sorted_growth_kernel(
         a_banks[2, 0] = angles(2, 0)
         fracs[1, 0] = reduce_turns(*turns[1, 0])
         a_banks[2, 1] = angles(2, 1)
-        first_h_b = keep.tile([P, G, TOK, PACK], BF16, name="first_h_b", align_bytes=64)
-        h_b = first_h_b[:]
+        for g in range(G):
+            deal_w2(g)
+        h_b = w2_raw[G - 1][:, 0, :].bitcast(BF16).rearrange("p (g j t) -> p g j t", g=G, t=PACK)
         for i in range(TILES):
             if i >= 1:
                 growth(sums[i - 1], 1, *codes[i - 1])
@@ -330,7 +343,7 @@ def tile_list_tide_sorted_growth_kernel(
             quantise(h_w, h_s, 1, h_b)
             h_b = rounded(cosine)
             if i == 0:
-                deal_weights()
+                deal_w3()
             sums[i] = psum.tile([P, PACK, TOK], F32, name="d", bufs=2)
             growth(sums[i], 0, *codes[i])
             if i + 3 < TILES:
@@ -344,7 +357,7 @@ def tile_list_tide_sorted_growth_kernel(
         early = weigh_growth(TILES - 2, sums[TILES - 2], spent[0][:, :1], slice(0, 1))
         place(TILES - 2, early, range(1))
         d_sb = weigh_growth(TILES - 1, sums[TILES - 1], spent[1])
-        last_wgo = wgo_t[S // WGO_COLS - 1][:, :, WGO_COLS - TOK :]
+        last_wgo = wgo_t[TILES - 1]
         weigh_growth(TILES - 2, sums[TILES - 2], last_wgo[:, 1:], slice(1, PACK))
 
         y_rows = out_0.rearrange("(p t) m -> t p m", t=PACK)

@@ -56,34 +56,36 @@ def tile_list_tide_sorted_growth_kernel(
         tab_w = [keep.tile([P, T], U32, name="tab_w%d" % a, align_bytes=64) for a in range(G)]
         tab_s = keep.tile([P, T], U8, name="tab_s", align_bytes=64)
         w1_w = [keep.tile([P, G, PASS], U32, name="w1_w%d" % g, align_bytes=64) for g in range(G)]
-        w1_s = keep.tile([P, H], U8, name="w1_s", align_bytes=64)
+        w1_s = keep.tile([P, G, H], U8, name="w1_s", align_bytes=64)
         w3_s_raw = keep.tile([P, G, N], U8, name="w3_s_raw", align_bytes=64)
         ident = keep.tile([P, P], F32, name="ident")
         minus_base = keep.tile([P, P], F32, name="minus_base")
 
         nc.gpsimd.memset(tab_s[:].bitcast(I32), 0)
-        nc.gpsimd.memset(w1_s[:].bitcast(I32), 0)
         make_identity(nc, ident[:])
+        nc.vector.memset(w1_s[:].rearrange("p g n -> p (g n)").bitcast(I32), 0)
         nc.vector.memset(minus_base[:], -TURN_BASE)
         nc.vector.memset(w3_s_raw[:].rearrange("p g n -> p (g n)").bitcast(I32), 0)
 
         def load_words(dst, words):
             nc.sync.dma_start(out=dst.bitcast(I32), in_=words.rearrange("p c i -> p (c i)").bitcast(I32))
 
-        def load_scales(dst, scales, q):
-            nc.sync.dma_start(
-                out=dst[32 * q : 32 * q + 4 * G, :].bitcast(I32), in_=scales[:, 4 * q : 4 * q + 4, :].bitcast(I32)
-            )
+        def load_scales(dst, scales, quads):
+            for q in quads:
+                nc.sync.dma_start(
+                    out=dst[32 * q : 32 * q + 4].bitcast(I32),
+                    in_=scales[:, 4 * q : 4 * q + 4, :].rearrange("g r n -> r g n").bitcast(I32),
+                )
 
         nc.sync.dma_start(idx[:], offs)
         load_words(tab_w[0][:], tab_words[0])
         for q in range(QUADS):
-            load_scales(tab_s, tab_scales, q)
-        for q in range(QUADS // 2):
-            load_scales(w1_s, w1_scales, q)
+            nc.sync.dma_start(
+                out=tab_s[32 * q : 32 * q + 4 * G, :].bitcast(I32), in_=tab_scales[:, 4 * q : 4 * q + 4, :].bitcast(I32)
+            )
+        load_scales(w1_s, w1_scales, range(QUADS // 2))
         load_words(tab_w[1][:], tab_words[1])
-        for q in range(QUADS // 2, QUADS):
-            load_scales(w1_s, w1_scales, q)
+        load_scales(w1_s, w1_scales, range(QUADS // 2, QUADS))
         w1_cols = w1_words.rearrange("a p c i -> p a (c i)").bitcast(I32)
         for g in range(G):
             nc.sync.dma_start(out=w1_w[g][:].bitcast(I32), in_=w1_cols[:, :, PASS * g : PASS * (g + 1)])
@@ -102,25 +104,21 @@ def tile_list_tide_sorted_growth_kernel(
 
         def load_wgo(lo, hi):
             piece = keep.tile([P, PACK, hi - lo], F32, name="wgo%d" % lo)
-            for q in range(QUADS):
+            for q in (0, 2, 1, 3):
                 nc.sync.dma_start(out=piece[32 * q : 32 * q + 32], in_=wgo_rows[:, :, lo:hi])
             for i in range(lo // TOK, hi // TOK):
                 wgo_t[i] = piece[:, :, i * TOK - lo : (i + 1) * TOK - lo]
 
         w2_raw = [keep.tile([P, PACK, N], F32, name="w2_raw%d" % g, align_bytes=64) for g in range(G)]
         w2_rows = w2.rearrange("(g p j) n -> g p j n", g=G, j=PACK)
-        for g in range(G):
-            nc.sync.dma_start(out=w2_raw[g][:], in_=w2_rows[g])
+        nc.sync.dma_start(out=w2_raw[0][:], in_=w2_rows[0])
         load_amp(0)
+        nc.sync.dma_start(out=w2_raw[1][:], in_=w2_rows[1])
         gc_t = keep.tile([P, G, PACK], F32, name="gc_t")
         nc.sync.dma_start(out=gc_t[:], in_=gc.rearrange("(g p t) -> p g t", g=G, t=PACK))
         w3_w_raw = keep.tile([P, G, 2 * N], U8, name="w3_w_raw", align_bytes=64)
         nc.sync.dma_start(out=w3_w_raw[:].bitcast(I32), in_=w3_words.rearrange("g p b -> p g b").bitcast(I32))
-        for q in range(QUADS):
-            nc.sync.dma_start(
-                out=w3_s_raw[32 * q : 32 * q + 4].bitcast(I32),
-                in_=w3_scales[:, 4 * q : 4 * q + 4, :].rearrange("g r n -> r g n").bitcast(I32),
-            )
+        load_scales(w3_s_raw, w3_scales, range(QUADS))
         load_wgo(*WGO_PARTS[0])
         nc.sync.dma_start(idx2[:], offs2)
         load_amp(1)
@@ -138,17 +136,19 @@ def tile_list_tide_sorted_growth_kernel(
             for i in range(lo // TOK, hi // TOK):
                 picked[key, i] = dst[:, at + i * TOK - lo : at + (i + 1) * TOK - lo]
 
-        v_first = keep.tile([P, S], U32, name="v_first", align_bytes=64)
+        v_first = keep.tile([P, 2 * GATHER], U32, name="v_first", align_bytes=64)
+        v_head = keep.tile([P, GATHER + TOK], U32, name="v_head", align_bytes=64)
         v_second = keep.tile([P, S // 2 + TOK], U32, name="v_second", align_bytes=64)
         v_next = keep.tile([P, GATHER], U32, name="v_next", align_bytes=64)
         v_s = keep.tile([P, S - GATHER + TOK], U8, name="v_s", align_bytes=64)
-        look_up(0, tab_w[0], v_first, 0, S)
+        look_up(0, tab_w[0], v_head, 0, GATHER, at=TOK)
         look_up("s", tab_s, v_s, 0, GATHER, at=S - GATHER - TOK)
+        look_up(0, tab_w[0], v_first, GATHER, 3 * GATHER)
         look_up(1, tab_w[1], v_second, 0, GATHER, at=S // 2 - TOK)
         look_up(1, tab_w[1], v_next, GATHER, 2 * GATHER)
 
         warm = keep.tile([P, 1], F32, name="warm")
-        nc.scalar.activation(out=warm[:], in_=ident[:, 0:1], func=ACT.Sin)
+        nc.scalar.activation(out=warm[:], in_=minus_base[:, 0:1], func=ACT.Sin, scale=0.0)
 
         w2_w = keep.tile([P, G, N], U32, name="w2_w", align_bytes=64)
         w2_s = keep.tile([P, G, N], U8, name="w2_s", align_bytes=64)
@@ -188,7 +188,7 @@ def tile_list_tide_sorted_growth_kernel(
                     lhsT=picked[a, i].bitcast(FP8X4),
                     lhsT_scale=picked["s", i][4 * a :, :],
                     rhs=w1_w[g][:, a, :].bitcast(FP8X4),
-                    rhs_scale=w1_s[4 * a :, PASS * g : PASS * (g + 1)],
+                    rhs_scale=w1_s[:, a, PASS * g : PASS * (g + 1)],
                     start=(a == 0),
                     stop=(a == G - 1),
                 )
@@ -309,6 +309,7 @@ def tile_list_tide_sorted_growth_kernel(
             if i == 0:
                 look_up("s", tab_s, v_s, GATHER, S)
                 look_up(1, tab_w[1], v_second, 2 * GATHER, S)
+                look_up(0, tab_w[0], v_head, 3 * GATHER, S)
             both = [to_turns(a_banks[i, g]) for g in range(G)]
             for g in range(G):
                 turns[i, g] = to_whole(i, both[g])
@@ -317,9 +318,8 @@ def tile_list_tide_sorted_growth_kernel(
         a_banks[2, 0] = angles(2, 0)
         fracs[1, 0] = reduce_turns(*turns[1, 0])
         a_banks[2, 1] = angles(2, 1)
-        for g in range(G):
-            deal_w2(g)
-        h_b = w2_raw[G - 1][:, 0, :].bitcast(BF16).rearrange("p (g j t) -> p g j t", g=G, t=PACK)
+        deal_w2(0)
+        h_b = w2_raw[0][:, 0, :].bitcast(BF16).rearrange("p (g j t) -> p g j t", g=G, t=PACK)
         for i in range(TILES):
             if i >= 1:
                 growth(sums[i - 1], 1, *codes[i - 1])
@@ -343,6 +343,7 @@ def tile_list_tide_sorted_growth_kernel(
             quantise(h_w, h_s, 1, h_b)
             h_b = rounded(cosine)
             if i == 0:
+                h_b = deal_w2(1)[:, :G]
                 deal_w3()
             sums[i] = psum.tile([P, PACK, TOK], F32, name="d", bufs=2)
             growth(sums[i], 0, *codes[i])
@@ -374,22 +375,32 @@ def tile_list_tide_sorted_growth_kernel(
         finish(nc.gpsimd, 1, slice(0, S))
         place(TILES - 2, last_wgo, (3,))
         place(TILES - 1, d_sb, (2, 3))
-        finish(nc.vector, 2, slice(0, S))
 
-        halves = (slice(0, S // 2), slice(S // 2, S))
+        quarter = S // 4
         y_w = keep.tile([P, S], U32, name="y_w", align_bytes=64)
         y_s = keep.tile([P, S], U8, name="y_s", align_bytes=64)
-        y_b = [keep.tile([P, S // 2, PACK], BF16, name="y_b%d" % h, align_bytes=64) for h in range(2)]
-        for cols in halves:
-            finish(nc.vector, PACK - 1, cols)
-        for y_half, cols, copy in zip(y_b, halves, (nc.scalar.copy, nc.vector.tensor_copy)):
+        y_b = [keep.tile([P, n * quarter, PACK], BF16, name="y_b%d" % h, align_bytes=64) for h, n in enumerate((2, 1, 1))]
+        rounded_q = [y_b[0][:, :quarter], y_b[0][:, quarter:], y_b[1][:], y_b[2][:]]
+        y_pairs = out_0.rearrange("(p t) m -> p t m", t=PACK)
+        for n, c in enumerate((0, 1, 3, 2)):
+            cols = slice(c * quarter, (c + 1) * quarter)
+            for t in (2, 3):
+                y_t = y_all[:, t, :][:, cols]
+                nc.vector.tensor_tensor(out=y_t, in0=page[t][:, cols], in1=y_t, op=ALU.mult)
+            if n % 2:
+                half = slice(n // 2 * S // 2, (n // 2 + 1) * S // 2)
+                nc.sync.dma_start(out=y_pairs[:, 2:, half], in_=y_all[:, 2:, half])
+        for c in range(4):
+            cols = slice(c * quarter, (c + 1) * quarter)
+            copy = nc.vector.tensor_copy if c == 3 else nc.scalar.copy
             copy(
-                out=y_half[:].rearrange("p (c i) t -> p c t i", i=RUN),
+                out=rounded_q[c].rearrange("p (c i) t -> p c t i", i=RUN),
                 in_=y_all[:, :, cols].rearrange("p t (c i) -> p c t i", i=RUN),
             )
-        for y_half, cols in reversed(list(zip(y_b, halves))):
+        for h, lo, hi in ((0, 0, 2), (2, 3, 4), (1, 2, 3)):
+            cols = slice(lo * quarter, hi * quarter)
             nc.vector.quantize_mx(
-                out=y_w[:, cols].bitcast(FP8X4), scales=y_s[:, cols], in_=y_half[:].rearrange("p c t -> p (c t)")
+                out=y_w[:, cols].bitcast(FP8X4), scales=y_s[:, cols], in_=y_b[h][:].rearrange("p c t -> p (c t)")
             )
             nc.sync.dma_start(
                 out=out_1[0][:, cols, :].rearrange("p c i -> p (c i)").bitcast(I32), in_=y_w[:, cols].bitcast(I32)

@@ -61,7 +61,7 @@ def tile_list_tide_sorted_growth_kernel(
         ident = keep.tile([P, P], F32, name="ident")
         minus_base = keep.tile([P, P], F32, name="minus_base")
 
-        nc.gpsimd.memset(tab_s[:].bitcast(I32), 0)
+        nc.vector.memset(tab_s[:].bitcast(I32), 0)
         make_identity(nc, ident[:])
         nc.vector.memset(w1_s[:].rearrange("p g n -> p (g n)").bitcast(I32), 0)
         nc.vector.memset(minus_base[:], -TURN_BASE)
@@ -78,14 +78,16 @@ def tile_list_tide_sorted_growth_kernel(
                 )
 
         nc.sync.dma_start(idx[:], offs)
-        load_words(tab_w[0][:], tab_words[0])
+        nc.sync.dma_start(idx2[:], offs2)
+        gc_t = keep.tile([P, G, PACK], F32, name="gc_t")
+        nc.sync.dma_start(out=gc_t[:], in_=gc.rearrange("(g p t) -> p g t", g=G, t=PACK))
         for q in range(QUADS):
             nc.sync.dma_start(
                 out=tab_s[32 * q : 32 * q + 4 * G, :].bitcast(I32), in_=tab_scales[:, 4 * q : 4 * q + 4, :].bitcast(I32)
             )
-        load_scales(w1_s, w1_scales, range(QUADS // 2))
-        load_words(tab_w[1][:], tab_words[1])
-        load_scales(w1_s, w1_scales, range(QUADS // 2, QUADS))
+        for a in range(G):
+            load_words(tab_w[a][:], tab_words[a])
+        load_scales(w1_s, w1_scales, range(QUADS))
         w1_cols = w1_words.rearrange("a p c i -> p a (c i)").bitcast(I32)
         for g in range(G):
             nc.sync.dma_start(out=w1_w[g][:].bitcast(I32), in_=w1_cols[:, :, PASS * g : PASS * (g + 1)])
@@ -112,15 +114,12 @@ def tile_list_tide_sorted_growth_kernel(
         w2_raw = [keep.tile([P, PACK, N], F32, name="w2_raw%d" % g, align_bytes=64) for g in range(G)]
         w2_rows = w2.rearrange("(g p j) n -> g p j n", g=G, j=PACK)
         nc.sync.dma_start(out=w2_raw[0][:], in_=w2_rows[0])
-        load_amp(0)
         nc.sync.dma_start(out=w2_raw[1][:], in_=w2_rows[1])
-        gc_t = keep.tile([P, G, PACK], F32, name="gc_t")
-        nc.sync.dma_start(out=gc_t[:], in_=gc.rearrange("(g p t) -> p g t", g=G, t=PACK))
+        load_amp(0)
         w3_w_raw = keep.tile([P, G, 2 * N], U8, name="w3_w_raw", align_bytes=64)
         nc.sync.dma_start(out=w3_w_raw[:].bitcast(I32), in_=w3_words.rearrange("g p b -> p g b").bitcast(I32))
         load_scales(w3_s_raw, w3_scales, range(QUADS))
         load_wgo(*WGO_PARTS[0])
-        nc.sync.dma_start(idx2[:], offs2)
         load_amp(1)
         load_amp(2)
         load_wgo(*WGO_PARTS[1])
@@ -140,9 +139,9 @@ def tile_list_tide_sorted_growth_kernel(
         v_head = keep.tile([P, GATHER + TOK], U32, name="v_head", align_bytes=64)
         v_second = keep.tile([P, S // 2 + TOK], U32, name="v_second", align_bytes=64)
         v_next = keep.tile([P, GATHER], U32, name="v_next", align_bytes=64)
-        v_s = keep.tile([P, S - GATHER + TOK], U8, name="v_s", align_bytes=64)
+        v_s = keep.tile([P, S], U8, name="v_s", align_bytes=64)
+        look_up("s", tab_s, v_s, 0, S)
         look_up(0, tab_w[0], v_head, 0, GATHER, at=TOK)
-        look_up("s", tab_s, v_s, 0, GATHER, at=S - GATHER - TOK)
         look_up(0, tab_w[0], v_first, GATHER, 3 * GATHER)
         look_up(1, tab_w[1], v_second, 0, GATHER, at=S // 2 - TOK)
         look_up(1, tab_w[1], v_next, GATHER, 2 * GATHER)
@@ -307,7 +306,6 @@ def tile_list_tide_sorted_growth_kernel(
             for g in range(G):
                 a_banks[i, g] = angles(i, g)
             if i == 0:
-                look_up("s", tab_s, v_s, GATHER, S)
                 look_up(1, tab_w[1], v_second, 2 * GATHER, S)
                 look_up(0, tab_w[0], v_head, 3 * GATHER, S)
             both = [to_turns(a_banks[i, g]) for g in range(G)]
@@ -318,8 +316,9 @@ def tile_list_tide_sorted_growth_kernel(
         a_banks[2, 0] = angles(2, 0)
         fracs[1, 0] = reduce_turns(*turns[1, 0])
         a_banks[2, 1] = angles(2, 1)
-        deal_w2(0)
-        h_b = w2_raw[0][:, 0, :].bitcast(BF16).rearrange("p (g j t) -> p g j t", g=G, t=PACK)
+        for g in range(G):
+            deal_w2(g)
+        h_b = w2_raw[G - 1][:, 0, :].bitcast(BF16).rearrange("p (g j t) -> p g j t", g=G, t=PACK)
         for i in range(TILES):
             if i >= 1:
                 growth(sums[i - 1], 1, *codes[i - 1])
@@ -343,7 +342,6 @@ def tile_list_tide_sorted_growth_kernel(
             quantise(h_w, h_s, 1, h_b)
             h_b = rounded(cosine)
             if i == 0:
-                h_b = deal_w2(1)[:, :G]
                 deal_w3()
             sums[i] = psum.tile([P, PACK, TOK], F32, name="d", bufs=2)
             growth(sums[i], 0, *codes[i])
@@ -357,9 +355,10 @@ def tile_list_tide_sorted_growth_kernel(
         spent = [cosine[:, g].rearrange("p j t -> p (j t)").rearrange("p (t j) -> p t j", t=PACK) for g in range(G)]
         early = weigh_growth(TILES - 2, sums[TILES - 2], spent[0][:, :1], slice(0, 1))
         place(TILES - 2, early, range(1))
-        d_sb = weigh_growth(TILES - 1, sums[TILES - 1], spent[1])
+        d_sb = spent[1]
+        for rows in (slice(0, 1), slice(1, PACK)):
+            weigh_growth(TILES - 1, sums[TILES - 1], d_sb[:, rows], rows)
         last_wgo = wgo_t[TILES - 1]
-        weigh_growth(TILES - 2, sums[TILES - 2], last_wgo[:, 1:], slice(1, PACK))
 
         y_rows = out_0.rearrange("(p t) m -> t p m", t=PACK)
 
@@ -370,8 +369,9 @@ def tile_list_tide_sorted_growth_kernel(
 
         place(TILES - 1, d_sb, (0,))
         finish(nc.gpsimd, 0, slice(0, S))
-        place(TILES - 2, last_wgo, (1, 2))
+        weigh_growth(TILES - 2, sums[TILES - 2], last_wgo[:, 1:], slice(1, PACK))
         place(TILES - 1, d_sb, (1,))
+        place(TILES - 2, last_wgo, (2, 1))
         finish(nc.gpsimd, 1, slice(0, S))
         place(TILES - 2, last_wgo, (3,))
         place(TILES - 1, d_sb, (2, 3))

@@ -29,9 +29,9 @@ LIST_COL = 16
 RUN = 4
 PAIR = 2
 GATHER = 256
-AMP_COLS = 256
+AMP_PARTS = ((0, 128), (128, 256), (256, 512), (512, 768), (768, 1024))
 LAG = 2
-ROUNDED_ON_VECTOR = (2, 3)
+ROUNDED_ON_VECTOR = (1, 2)
 WGO_PARTS = ((0, 512), (512, 1024))
 
 TURN_BASE = 98304.0
@@ -55,7 +55,8 @@ def tile_list_tide_sorted_growth_kernel(
 
         tab_w = [keep.tile([P, T], U32, name="tab_w%d" % a, align_bytes=64) for a in range(G)]
         tab_s = keep.tile([P, T], U8, name="tab_s", align_bytes=64)
-        w1_w = [keep.tile([P, G, PASS], U32, name="w1_w%d" % g, align_bytes=64) for g in range(G)]
+        w1_first = [keep.tile([P, PASS], U32, name="w1_first%d" % a, align_bytes=64) for a in range(G)]
+        w1_second = keep.tile([P, G, PASS], U32, name="w1_second", align_bytes=64)
         w1_s = keep.tile([P, G, H], U8, name="w1_s", align_bytes=64)
         w3_s_raw = keep.tile([P, G, N], U8, name="w3_s_raw", align_bytes=64)
         ident = keep.tile([P, P], F32, name="ident")
@@ -85,21 +86,24 @@ def tile_list_tide_sorted_growth_kernel(
             nc.sync.dma_start(
                 out=tab_s[32 * q : 32 * q + 4 * G, :].bitcast(I32), in_=tab_scales[:, 4 * q : 4 * q + 4, :].bitcast(I32)
             )
-        for a in range(G):
-            load_words(tab_w[a][:], tab_words[a])
+        load_words(tab_w[0][:], tab_words[0])
         load_scales(w1_s, w1_scales, range(QUADS))
         w1_cols = w1_words.rearrange("a p c i -> p a (c i)").bitcast(I32)
-        for g in range(G):
-            nc.sync.dma_start(out=w1_w[g][:].bitcast(I32), in_=w1_cols[:, :, PASS * g : PASS * (g + 1)])
+        nc.sync.dma_start(out=w1_first[0][:].bitcast(I32), in_=w1_cols[:, 0, :PASS])
+        load_words(tab_w[1][:], tab_words[1])
+        nc.sync.dma_start(out=w1_first[1][:].bitcast(I32), in_=w1_cols[:, 1, :PASS])
+        nc.sync.dma_start(out=w1_second[:].bitcast(I32), in_=w1_cols[:, :, PASS:])
 
         amp_rows = amp.rearrange("(g p t) j -> g p t j", g=G, t=PACK)
         amp_t = {}
 
         def load_amp(part):
+            lo, hi = AMP_PARTS[part]
             for g in range(G):
-                piece = keep.tile([P, PACK, AMP_COLS], F32, name="amp%d_%d" % (part, g))
-                nc.sync.dma_start(out=piece[:], in_=amp_rows[g][:, :, part * AMP_COLS : (part + 1) * AMP_COLS])
-                amp_t[part, g] = piece
+                piece = keep.tile([P, PACK, hi - lo], F32, name="amp%d_%d" % (part, g))
+                nc.sync.dma_start(out=piece[:], in_=amp_rows[g][:, :, lo:hi])
+                for i in range(lo // TOK, hi // TOK):
+                    amp_t[i, g] = piece[:, :, i * TOK - lo : (i + 1) * TOK - lo]
 
         wgo_rows = wgo.rearrange("(q t) j -> q t j", t=PACK)
         wgo_t = {}
@@ -114,16 +118,17 @@ def tile_list_tide_sorted_growth_kernel(
         w2_raw = [keep.tile([P, PACK, N], F32, name="w2_raw%d" % g, align_bytes=64) for g in range(G)]
         w2_rows = w2.rearrange("(g p j) n -> g p j n", g=G, j=PACK)
         nc.sync.dma_start(out=w2_raw[0][:], in_=w2_rows[0])
-        nc.sync.dma_start(out=w2_raw[1][:], in_=w2_rows[1])
         load_amp(0)
+        nc.sync.dma_start(out=w2_raw[1][:], in_=w2_rows[1])
+        load_amp(1)
         w3_w_raw = keep.tile([P, G, 2 * N], U8, name="w3_w_raw", align_bytes=64)
         nc.sync.dma_start(out=w3_w_raw[:].bitcast(I32), in_=w3_words.rearrange("g p b -> p g b").bitcast(I32))
         load_scales(w3_s_raw, w3_scales, range(QUADS))
         load_wgo(*WGO_PARTS[0])
-        load_amp(1)
         load_amp(2)
-        load_wgo(*WGO_PARTS[1])
         load_amp(3)
+        load_wgo(*WGO_PARTS[1])
+        load_amp(4)
         y_all = keep.tile([P, PACK, S], F32, name="y_all")
         nc.sync.dma_start(out=y_all[:], in_=x0.rearrange("(p t) m -> p t m", t=PACK))
 
@@ -186,7 +191,7 @@ def tile_list_tide_sorted_growth_kernel(
                     out=a_t[:],
                     lhsT=picked[a, i].bitcast(FP8X4),
                     lhsT_scale=picked["s", i][4 * a :, :],
-                    rhs=w1_w[g][:, a, :].bitcast(FP8X4),
+                    rhs=(w1_second[:, a, :] if g else w1_first[a][:]).bitcast(FP8X4),
                     rhs_scale=w1_s[:, a, PASS * g : PASS * (g + 1)],
                     start=(a == 0),
                     stop=(a == G - 1),
@@ -201,10 +206,13 @@ def tile_list_tide_sorted_growth_kernel(
             )
             return turns
 
-        def to_whole(i, turns):
-            whole = ring.tile([P, PACK, P], U32, name="whole", bufs=6)
+        def to_whole(i, g, turns):
+            if i == 1:
+                whole = w2_raw[0][:, g, :].bitcast(U32).rearrange("j (t p) -> j t p", t=PACK)
+            else:
+                whole = ring.tile([P, PACK, P], U32, name="whole", bufs=6)[:]
             src = turns[:].rearrange("j t p -> j (t p)")
-            dst = whole[:].rearrange("j t p -> j (t p)")
+            dst = whole.rearrange("j t p -> j (t p)")
             if i in ROUNDED_ON_VECTOR:
                 nc.vector.tensor_scalar(
                     out=dst.bitcast(I32), in0=src, scalar1=-TURN_STEP, scalar2=TURN_BITS, op0=ALU.mult, op1=ALU.add
@@ -251,12 +259,11 @@ def tile_list_tide_sorted_growth_kernel(
             )
 
         def weigh_sine(i, sine, h_b):
-            part, lo = divmod(i * TOK, AMP_COLS)
             for g in reversed(range(G)):
                 nc.vector.tensor_tensor(
                     out=h_b[:, g].rearrange("p (c i) t -> p c t i", i=PAIR),
                     in0=sine[:, g].rearrange("p t j -> p (t j)").rearrange("p (c t i) -> p c t i", t=PACK, i=PAIR),
-                    in1=amp_t[part, g][:, :, lo : lo + TOK].rearrange("p t (c i) -> p c t i", i=PAIR),
+                    in1=amp_t[i, g].rearrange("p t (c i) -> p c t i", i=PAIR),
                     op=ALU.mult,
                 )
 
@@ -308,17 +315,20 @@ def tile_list_tide_sorted_growth_kernel(
             if i == 0:
                 look_up(1, tab_w[1], v_second, 2 * GATHER, S)
                 look_up(0, tab_w[0], v_head, 3 * GATHER, S)
-            both = [to_turns(a_banks[i, g]) for g in range(G)]
-            for g in range(G):
-                turns[i, g] = to_whole(i, both[g])
+            if i == 0:
+                for g in range(G):
+                    turns[i, g] = to_whole(i, g, to_turns(a_banks[i, g]))
+            else:
+                deal_w2(0)
+                both = [to_turns(a_banks[i, g]) for g in range(G)]
+                for g in range(G):
+                    turns[i, g] = to_whole(i, g, both[g])
         for g in range(G):
             fracs[0, g] = reduce_turns(*turns[0, g])
         a_banks[2, 0] = angles(2, 0)
         fracs[1, 0] = reduce_turns(*turns[1, 0])
         a_banks[2, 1] = angles(2, 1)
-        for g in range(G):
-            deal_w2(g)
-        h_b = w2_raw[G - 1][:, 0, :].bitcast(BF16).rearrange("p (g j t) -> p g j t", g=G, t=PACK)
+        h_b = w2_raw[0][:, G, :].bitcast(BF16).rearrange("p (g j t) -> p g j t", g=G, t=PACK)
         for i in range(TILES):
             if i >= 1:
                 growth(sums[i - 1], 1, *codes[i - 1])
@@ -328,7 +338,7 @@ def tile_list_tide_sorted_growth_kernel(
             if i + 2 < TILES:
                 both = [to_turns(a_banks[i + 2, g]) for g in range(G)]
                 for g in range(G):
-                    turns[i + 2, g] = to_whole(i + 2, both[g])
+                    turns[i + 2, g] = to_whole(i + 2, g, both[g])
             h_w = ring.tile([P, 2 * G * TOK], U32, name="h_w", align_bytes=64)
             h_s = ring.tile([P, 2 * G * TOK], U8, name="h_s", align_bytes=64)
             codes[i] = (h_w, h_s)
@@ -342,6 +352,7 @@ def tile_list_tide_sorted_growth_kernel(
             quantise(h_w, h_s, 1, h_b)
             h_b = rounded(cosine)
             if i == 0:
+                h_b = deal_w2(1)[:, :G]
                 deal_w3()
             sums[i] = psum.tile([P, PACK, TOK], F32, name="d", bufs=2)
             growth(sums[i], 0, *codes[i])

@@ -29,9 +29,9 @@ LIST_COL = 16
 RUN = 4
 PAIR = 2
 GATHER = 256
-AMP_PARTS = ((0, 128), (128, 256), (256, 512), (512, 768), (768, 1024))
+AMP_PARTS = ((0, 256), (256, 512), (512, 768), (768, 1024))
 LAG = 2
-ROUNDED_ON_VECTOR = (1, 2)
+ROUNDED_ON_VECTOR = (2, 3)
 WGO_PARTS = ((0, 512), (512, 1024))
 
 TURN_BASE = 98304.0
@@ -80,17 +80,15 @@ def tile_list_tide_sorted_growth_kernel(
 
         nc.sync.dma_start(idx[:], offs)
         nc.sync.dma_start(idx2[:], offs2)
-        gc_t = keep.tile([P, G, PACK], F32, name="gc_t")
-        nc.sync.dma_start(out=gc_t[:], in_=gc.rearrange("(g p t) -> p g t", g=G, t=PACK))
         for q in range(QUADS):
             nc.sync.dma_start(
                 out=tab_s[32 * q : 32 * q + 4 * G, :].bitcast(I32), in_=tab_scales[:, 4 * q : 4 * q + 4, :].bitcast(I32)
             )
         load_words(tab_w[0][:], tab_words[0])
-        load_scales(w1_s, w1_scales, range(QUADS))
         w1_cols = w1_words.rearrange("a p c i -> p a (c i)").bitcast(I32)
         nc.sync.dma_start(out=w1_first[0][:].bitcast(I32), in_=w1_cols[:, 0, :PASS])
         load_words(tab_w[1][:], tab_words[1])
+        load_scales(w1_s, w1_scales, range(QUADS))
         nc.sync.dma_start(out=w1_first[1][:].bitcast(I32), in_=w1_cols[:, 1, :PASS])
         nc.sync.dma_start(out=w1_second[:].bitcast(I32), in_=w1_cols[:, :, PASS:])
 
@@ -118,17 +116,18 @@ def tile_list_tide_sorted_growth_kernel(
         w2_raw = [keep.tile([P, PACK, N], F32, name="w2_raw%d" % g, align_bytes=64) for g in range(G)]
         w2_rows = w2.rearrange("(g p j) n -> g p j n", g=G, j=PACK)
         nc.sync.dma_start(out=w2_raw[0][:], in_=w2_rows[0])
-        load_amp(0)
         nc.sync.dma_start(out=w2_raw[1][:], in_=w2_rows[1])
-        load_amp(1)
+        load_amp(0)
+        gc_t = keep.tile([P, G, PACK], F32, name="gc_t")
+        nc.sync.dma_start(out=gc_t[:], in_=gc.rearrange("(g p t) -> p g t", g=G, t=PACK))
         w3_w_raw = keep.tile([P, G, 2 * N], U8, name="w3_w_raw", align_bytes=64)
         nc.sync.dma_start(out=w3_w_raw[:].bitcast(I32), in_=w3_words.rearrange("g p b -> p g b").bitcast(I32))
         load_scales(w3_s_raw, w3_scales, range(QUADS))
         load_wgo(*WGO_PARTS[0])
+        load_amp(1)
         load_amp(2)
-        load_amp(3)
         load_wgo(*WGO_PARTS[1])
-        load_amp(4)
+        load_amp(3)
         y_all = keep.tile([P, PACK, S], F32, name="y_all")
         nc.sync.dma_start(out=y_all[:], in_=x0.rearrange("(p t) m -> p t m", t=PACK))
 
@@ -207,10 +206,7 @@ def tile_list_tide_sorted_growth_kernel(
             return turns
 
         def to_whole(i, g, turns):
-            if i == 1:
-                whole = w2_raw[0][:, g, :].bitcast(U32).rearrange("j (t p) -> j t p", t=PACK)
-            else:
-                whole = ring.tile([P, PACK, P], U32, name="whole", bufs=6)[:]
+            whole = ring.tile([P, PACK, P], U32, name="whole", bufs=6)[:]
             src = turns[:].rearrange("j t p -> j (t p)")
             dst = whole.rearrange("j t p -> j (t p)")
             if i in ROUNDED_ON_VECTOR:
@@ -319,7 +315,6 @@ def tile_list_tide_sorted_growth_kernel(
                 for g in range(G):
                     turns[i, g] = to_whole(i, g, to_turns(a_banks[i, g]))
             else:
-                deal_w2(0)
                 both = [to_turns(a_banks[i, g]) for g in range(G)]
                 for g in range(G):
                     turns[i, g] = to_whole(i, g, both[g])
@@ -328,7 +323,9 @@ def tile_list_tide_sorted_growth_kernel(
         a_banks[2, 0] = angles(2, 0)
         fracs[1, 0] = reduce_turns(*turns[1, 0])
         a_banks[2, 1] = angles(2, 1)
-        h_b = w2_raw[0][:, G, :].bitcast(BF16).rearrange("p (g j t) -> p g j t", g=G, t=PACK)
+        for g in range(G):
+            deal_w2(g)
+        h_b = w2_raw[G - 1][:, 0, :].bitcast(BF16).rearrange("p (g j t) -> p g j t", g=G, t=PACK)
         for i in range(TILES):
             if i >= 1:
                 growth(sums[i - 1], 1, *codes[i - 1])
@@ -352,7 +349,6 @@ def tile_list_tide_sorted_growth_kernel(
             quantise(h_w, h_s, 1, h_b)
             h_b = rounded(cosine)
             if i == 0:
-                h_b = deal_w2(1)[:, :G]
                 deal_w3()
             sums[i] = psum.tile([P, PACK, TOK], F32, name="d", bufs=2)
             growth(sums[i], 0, *codes[i])

@@ -209,8 +209,8 @@ def tile_list_tide_sorted_growth_kernel(
             whole = ring.tile([P, PACK, P], U32, name="whole", bufs=6)[:]
             src = turns[:].rearrange("j t p -> j (t p)")
             dst = whole.rearrange("j t p -> j (t p)")
-            if i in ROUNDED_ON_VECTOR:
-                nc.vector.tensor_scalar(
+            if i == 0 or i in ROUNDED_ON_VECTOR:
+                (nc.vector if i else nc.gpsimd).tensor_scalar(
                     out=dst.bitcast(I32), in0=src, scalar1=-TURN_STEP, scalar2=TURN_BITS, op0=ALU.mult, op1=ALU.add
                 )
             else:
@@ -413,6 +413,6 @@ def tile_list_tide_sorted_growth_kernel(
                 out=out_1[0][:, cols, :].rearrange("p c i -> p (c i)").bitcast(I32), in_=y_w[:, cols].bitcast(I32)
             )
         for q in range(QUADS):
-            nc.scalar.dma_start(
+            (nc.sync if q % 2 else nc.scalar).dma_start(
                 out=out_2[0][4 * q : 4 * q + 4, :].bitcast(I32), in_=y_s[32 * q : 32 * q + 4, :].bitcast(I32)
             )

import math
from contextlib import ExitStack

import concourse.mybir as mybir
from concourse.masks import make_identity

K, T, S, H, N = 1024, 2048, 1024, 1024, 512
FLOPS = 2 * K * H * S + 2 * 2 * H * N * S

F32 = mybir.dt.float32
BF16 = mybir.dt.bfloat16
I32 = mybir.dt.int32
U32 = mybir.dt.uint32
U16 = mybir.dt.uint16
U8 = mybir.dt.uint8
FP8X4 = mybir.dt.float8_e4m3fn_x4
FP4X4 = mybir.dt.float4_e2m1fn_x4
ACT = mybir.ActivationFunctionType
ALU = mybir.AluOpType

P = 128
PACK = 4
PASS = P * PACK
G = 2
QUADS = 4
TOK = 128
TILES = S // TOK
LIST_COL = 16
RUN = 4
PAIR = 2
GATHER = 256
AMP_PARTS = ((0, 256), (256, 512), (512, 768), (768, 1024))
LAG = 2
ROUNDED_ON_VECTOR = (2, 3)
WGO_PARTS = ((0, 512), (512, 1024))

TURN_BASE = 98304.0
TURN_BITS = 1203765248.0
TURN_STEP = 128.0


def tile_list_tide_sorted_growth_kernel(
    tc, tab_words, tab_scales, offs, offs2, w1_words, w1_scales, w2, w3_words, w3_scales, amp, gc, wgo, x0,
    out_0, out_1, out_2,
):
    nc = tc.nc
    with ExitStack() as ctx:
        lists = ctx.enter_context(tc.tile_pool(name="lists", bufs=1))
        keep = ctx.enter_context(tc.tile_pool(name="keep", bufs=1))
        ring = ctx.enter_context(tc.tile_pool(name="ring", bufs=2))
        psum = ctx.enter_context(tc.psum_pool(name="psum", bufs=2))

        idx = lists.tile([P, S // LIST_COL], U16, name="idx")
        idx2 = lists.tile([P, S // LIST_COL], U16, name="idx2")

        tab_w = [keep.tile([P, T], U32, name="tab_w%d" % a, align_bytes=64) for a in range(G)]
        tab_s = keep.tile([P, T], U8, name="tab_s", align_bytes=64)
        w1_first = [keep.tile([P, PASS], U32, name="w1_first%d" % a, align_bytes=64) for a in range(G)]
        w1_second = keep.tile([P, G, PASS], U32, name="w1_second", align_bytes=64)
        w1_s = keep.tile([P, G, H], U8, name="w1_s", align_bytes=64)
        w3_s_raw = keep.tile([P, G, N], U8, name="w3_s_raw", align_bytes=64)
        ident = keep.tile([P, P], F32, name="ident")
        minus_base = keep.tile([P, P], F32, name="minus_base")

        nc.vector.memset(tab_s[:].bitcast(I32), 0)
        make_identity(nc, ident[:])
        nc.vector.memset(w1_s[:].rearrange("p g n -> p (g n)").bitcast(I32), 0)
        nc.vector.memset(minus_base[:], -TURN_BASE)
        nc.vector.memset(w3_s_raw[:].rearrange("p g n -> p (g n)").bitcast(I32), 0)

        def load_words(dst, words):
            nc.sync.dma_start(out=dst.bitcast(I32), in_=words.rearrange("p c i -> p (c i)").bitcast(I32))

        def load_scales(dst, scales, quads):
            for q in quads:
                nc.sync.dma_start(
                    out=dst[32 * q : 32 * q + 4].bitcast(I32),
                    in_=scales[:, 4 * q : 4 * q + 4, :].rearrange("g r n -> r g n").bitcast(I32),
                )

        nc.sync.dma_start(idx[:], offs)
        nc.sync.dma_start(idx2[:], offs2)
        for q in range(QUADS):
            nc.sync.dma_start(
                out=tab_s[32 * q : 32 * q + 4 * G, :].bitcast(I32), in_=tab_scales[:, 4 * q : 4 * q + 4, :].bitcast(I32)
            )
        load_words(tab_w[0][:], tab_words[0])
        w1_cols = w1_words.rearrange("a p c i -> p a (c i)").bitcast(I32)
        nc.sync.dma_start(out=w1_first[0][:].bitcast(I32), in_=w1_cols[:, 0, :PASS])
        load_words(tab_w[1][:], tab_words[1])
        load_scales(w1_s, w1_scales, range(QUADS))
        nc.sync.dma_start(out=w1_first[1][:].bitcast(I32), in_=w1_cols[:, 1, :PASS])
        nc.sync.dma_start(out=w1_second[:].bitcast(I32), in_=w1_cols[:, :, PASS:])

        amp_rows = amp.rearrange("(g p t) j -> g p t j", g=G, t=PACK)
        amp_t = {}

        def load_amp(part):
            lo, hi = AMP_PARTS[part]
            for g in range(G):
                piece = keep.tile([P, PACK, hi - lo], F32, name="amp%d_%d" % (part, g))
                nc.sync.dma_start(out=piece[:], in_=amp_rows[g][:, :, lo:hi])
                for i in range(lo // TOK, hi // TOK):
                    amp_t[i, g] = piece[:, :, i * TOK - lo : (i + 1) * TOK - lo]

        wgo_rows = wgo.rearrange("(q t) j -> q t j", t=PACK)
        wgo_t = {}

        def load_wgo(lo, hi):
            piece = keep.tile([P, PACK, hi - lo], F32, name="wgo%d" % lo)
            for q in (0, 2, 1, 3):
                nc.sync.dma_start(out=piece[32 * q : 32 * q + 32], in_=wgo_rows[:, :, lo:hi])
            for i in range(lo // TOK, hi // TOK):
                wgo_t[i] = piece[:, :, i * TOK - lo : (i + 1) * TOK - lo]

        w2_raw = [keep.tile([P, PACK, N], F32, name="w2_raw%d" % g, align_bytes=64) for g in range(G)]
        w2_rows = w2.rearrange("(g p j) n -> g p j n", g=G, j=PACK)
        nc.sync.dma_start(out=w2_raw[0][:], in_=w2_rows[0])
        nc.sync.dma_start(out=w2_raw[1][:], in_=w2_rows[1])
        load_amp(0)
        gc_t = keep.tile([P, G, PACK], F32, name="gc_t")
        nc.sync.dma_start(out=gc_t[:], in_=gc.rearrange("(g p t) -> p g t", g=G, t=PACK))
        w3_w_raw = keep.tile([P, G, 2 * N], U8, name="w3_w_raw", align_bytes=64)
        nc.sync.dma_start(out=w3_w_raw[:].bitcast(I32), in_=w3_words.rearrange("g p b -> p g b").bitcast(I32))
        load_scales(w3_s_raw, w3_scales, range(QUADS))
        load_wgo(*WGO_PARTS[0])
        load_amp(1)
        load_amp(2)
        load_wgo(*WGO_PARTS[1])
        load_amp(3)
        y_all = keep.tile([P, PACK, S], F32, name="y_all")
        nc.sync.dma_start(out=y_all[:], in_=x0.rearrange("(p t) m -> p t m", t=PACK))

        picked = {}

        def look_up(key, window, dst, lo, hi, at=0):
            offsets = idx[:, lo // LIST_COL : hi // LIST_COL]
            nc.vector.tensor_copy(out=dst[:, at : at + hi - lo], in_=window[:].indirect(offsets))
            for i in range(lo // TOK, hi // TOK):
                picked[key, i] = dst[:, at + i * TOK - lo : at + (i + 1) * TOK - lo]

        v_first = keep.tile([P, 2 * GATHER], U32, name="v_first", align_bytes=64)
        v_head = keep.tile([P, GATHER + TOK], U32, name="v_head", align_bytes=64)
        v_second = keep.tile([P, S // 2 + TOK], U32, name="v_second", align_bytes=64)
        v_next = keep.tile([P, GATHER], U32, name="v_next", align_bytes=64)
        v_s = keep.tile([P, S], U8, name="v_s", align_bytes=64)
        look_up("s", tab_s, v_s, 0, S)
        look_up(0, tab_w[0], v_head, 0, GATHER, at=TOK)
        look_up(0, tab_w[0], v_first, GATHER, 3 * GATHER)
        look_up(1, tab_w[1], v_second, 0, GATHER, at=S // 2 - TOK)
        look_up(1, tab_w[1], v_next, GATHER, 2 * GATHER)

        warm = keep.tile([P, 1], F32, name="warm")
        nc.scalar.activation(out=warm[:], in_=minus_base[:, 0:1], func=ACT.Sin, scale=0.0)

        w2_w = keep.tile([P, G, N], U32, name="w2_w", align_bytes=64)
        w2_s = keep.tile([P, G, N], U8, name="w2_s", align_bytes=64)
        w3_w = keep.tile([P, G, 2 * N], U8, name="w3_w", align_bytes=64)
        w3_s = keep.tile([P, G, N], U8, name="w3_s", align_bytes=64)

        def deal_w2(g):
            w2_b = keep.tile([P, PACK, P, PACK], BF16, name="w2_b%d" % g, align_bytes=64)
            nc.vector.tensor_copy(
                out=w2_b[:].rearrange("p t m j -> p m t j"),
                in_=w2_raw[g][:].rearrange("p j (m t) -> p m t j", t=PACK),
            )
            nc.vector.quantize_mx(
                out=w2_w[:, g, :].bitcast(FP8X4),
                scales=w2_s[:, g, :],
                in_=w2_b[:].rearrange("p t m j -> p (t m j)"),
            )
            return w2_b

        def deal_w3():
            nc.vector.tensor_copy(
                out=w3_w[:].bitcast(U16).rearrange("p g (t m) -> p g t m", t=PACK),
                in_=w3_w_raw[:].bitcast(U16).rearrange("p g (m t) -> p g t m", t=PACK),
            )
            nc.vector.tensor_copy(
                out=w3_s[:].rearrange("p g (t m) -> p g t m", t=PACK),
                in_=w3_s_raw[:].rearrange("p g (m t) -> p g t m", t=PACK),
            )

        page = [keep.tile([P, S], F32, name="page%d" % t) for t in range(PACK)]

        def angles(i, g):
            a_t = psum.tile([P, PASS], F32, name="a_t", bufs=2)
            for a in range(G):
                nc.tensor.matmul_mx(
                    out=a_t[:],
                    lhsT=picked[a, i].bitcast(FP8X4),
                    lhsT_scale=picked["s", i][4 * a :, :],
                    rhs=(w1_second[:, a, :] if g else w1_first[a][:]).bitcast(FP8X4),
                    rhs_scale=w1_s[:, a, PASS * g : PASS * (g + 1)],
                    start=(a == 0),
                    stop=(a == G - 1),
                )
            return a_t

        def to_turns(bank):
            turns = ring.tile([P, PACK, P], F32, name="turns", bufs=6)
            nc.scalar.activation(
                out=turns[:], in_=bank[:].rearrange("j (p t) -> j t p", t=PACK), func=ACT.Copy,
                scale=1.0 / (2.0 * math.pi),
            )
            return turns

        def to_whole(i, g, turns):
            whole = ring.tile([P, PACK, P], U32, name="whole", bufs=6)[:]
            src = turns[:].rearrange("j t p -> j (t p)")
            dst = whole.rearrange("j t p -> j (t p)")
            if i == 0 or i in ROUNDED_ON_VECTOR:
                (nc.vector if i else nc.gpsimd).tensor_scalar(
                    out=dst.bitcast(I32), in0=src, scalar1=-TURN_STEP, scalar2=TURN_BITS, op0=ALU.mult, op1=ALU.add
                )
            else:
                nc.scalar.activation(out=dst, in_=src, func=ACT.Copy, scale=-TURN_STEP, bias=TURN_BITS)
            return turns, whole

        def reduce_turns(turns, whole):
            frac = psum.tile([P, PACK, TOK], F32, name="frac", bufs=3)
            for t in range(PACK):
                terms = (minus_base[:], whole[:, t, :].bitcast(F32), turns[:, t, :])
                for s, term in enumerate(terms):
                    nc.tensor.matmul(
                        out=frac[:, t, :], lhsT=term, rhs=ident[:], is_transpose=True,
                        start=(s == 0), stop=(s == len(terms) - 1),
                    )
            return frac

        def waves(banks):
            sine = ring.tile([P, G, PACK, TOK], F32, name="sine")
            cosine = ring.tile([P, G, TOK, PACK], F32, name="cosine", bufs=3, align_bytes=64)
            folded = ring.tile([P, G, TOK * PACK], F32, name="folded")
            for g in range(G):
                nc.scalar.activation(
                    out=sine[:, g].rearrange("p t j -> p (t j)").rearrange("p (c t i) -> p c t i", t=PACK, i=PAIR),
                    in_=banks[g][:].rearrange("p t (c i) -> p c t i", i=PAIR), func=ACT.Sin, scale=2.0 * math.pi,
                )
            for g in range(G):
                nc.scalar.activation(
                    out=folded[:, g].rearrange("p (j t) -> p j t", t=PACK),
                    in_=banks[g][:].rearrange("p t j -> p j t"), func=ACT.Abs,
                )
            for g in range(G):
                nc.scalar.activation(
                    out=cosine[:, g].rearrange("p j t -> p (j t)"), in_=folded[:, g],
                    func=ACT.Sin, scale=-2.0 * math.pi, bias=math.pi / 2.0,
                )
            return sine, cosine

        def rounded(cosine, half=0):
            return cosine[:, half].rearrange("p j t -> p (j t)").bitcast(BF16).rearrange(
                "p (g j t) -> p g j t", g=G, t=PACK
            )

        def weigh_sine(i, sine, h_b):
            for g in reversed(range(G)):
                nc.vector.tensor_tensor(
                    out=h_b[:, g].rearrange("p (c i) t -> p c t i", i=PAIR),
                    in0=sine[:, g].rearrange("p t j -> p (t j)").rearrange("p (c t i) -> p c t i", t=PACK, i=PAIR),
                    in1=amp_t[i, g].rearrange("p t (c i) -> p c t i", i=PAIR),
                    op=ALU.mult,
                )

        def weigh_cosine(i, cosine, h_b):
            engine = nc.gpsimd if i >= LAG else nc.vector
            engine.tensor_tensor(
                out=h_b, in0=cosine[:], in1=gc_t[:].unsqueeze(2).to_broadcast([P, G, TOK, PACK]), op=ALU.mult
            )

        def quantise(h_w, h_s, o, h_b):
            cols = slice(o * G * TOK, (o + 1) * G * TOK)
            nc.vector.quantize_mx(
                out=h_w[:, cols].bitcast(FP8X4), scales=h_s[:, cols],
                in_=h_b.rearrange("p g j t -> p (g j t)"),
            )

        def growth(d, o, h_w, h_s):
            for g in range(G):
                h_cols = slice((o * G + g) * TOK, (o * G + g + 1) * TOK)
                for t in range(PACK):
                    cols = slice(t * P, (t + 1) * P)
                    if o == 0:
                        w_w, w_s = w2_w[:, g, cols].bitcast(FP8X4), w2_s[:, g, cols]
                    else:
                        w_w, w_s = w3_w[:, g, 2 * t * P : 2 * (t + 1) * P].bitcast(FP4X4), w3_s[:, g, cols]
                    nc.tensor.matmul_mx(
                        out=d[:, t, :],
                        lhsT=w_w,
                        lhsT_scale=w_s,
                        rhs=h_w[:, h_cols].bitcast(FP8X4),
                        rhs_scale=h_s[:, h_cols],
                        start=(o, g, t) == (0, 0, 0),
                        stop=(o, g, t) == (1, G - 1, PACK - 1),
                    )

        def weigh_growth(i, d, scratch, rows=slice(0, PACK)):
            nc.vector.tensor_tensor(out=scratch, in0=d[:, rows], in1=wgo_t[i][:, rows], op=ALU.mult)
            return scratch

        def place(i, d_sb, rows):
            offsets = idx2[:, i * TOK // LIST_COL : (i + 1) * TOK // LIST_COL]
            for t in rows:
                nc.vector.tensor_copy(out=page[t][:].indirect(offsets), in_=d_sb[:, t, :])

        a_banks, turns, fracs, codes, sums = {}, {}, {}, {}, {}
        for i in range(2):
            for g in range(G):
                a_banks[i, g] = angles(i, g)
            if i == 0:
                look_up(1, tab_w[1], v_second, 2 * GATHER, S)
                look_up(0, tab_w[0], v_head, 3 * GATHER, S)
            if i == 0:
                for g in range(G):
                    turns[i, g] = to_whole(i, g, to_turns(a_banks[i, g]))
            else:
                both = [to_turns(a_banks[i, g]) for g in range(G)]
                for g in range(G):
                    turns[i, g] = to_whole(i, g, both[g])
        for g in range(G):
            fracs[0, g] = reduce_turns(*turns[0, g])
        a_banks[2, 0] = angles(2, 0)
        fracs[1, 0] = reduce_turns(*turns[1, 0])
        a_banks[2, 1] = angles(2, 1)
        for g in range(G):
            deal_w2(g)
        h_b = w2_raw[G - 1][:, 0, :].bitcast(BF16).rearrange("p (g j t) -> p g j t", g=G, t=PACK)
        for i in range(TILES):
            if i >= 1:
                growth(sums[i - 1], 1, *codes[i - 1])
            if i + 1 < TILES:
                fracs[i + 1, 1] = reduce_turns(*turns[i + 1, 1])
            sine, cosine = waves([fracs[i, g] for g in range(G)])
            if i + 2 < TILES:
                both = [to_turns(a_banks[i + 2, g]) for g in range(G)]
                for g in range(G):
                    turns[i + 2, g] = to_whole(i + 2, g, both[g])
            h_w = ring.tile([P, 2 * G * TOK], U32, name="h_w", align_bytes=64)
            h_s = ring.tile([P, 2 * G * TOK], U8, name="h_s", align_bytes=64)
            codes[i] = (h_w, h_s)
            weigh_sine(i, sine, h_b)
            if i >= LAG:
                d_sb = weigh_growth(i - LAG, sums[i - LAG], sine[:, G - 1])
            quantise(h_w, h_s, 0, h_b)
            weigh_cosine(i, cosine, h_b)
            if i >= LAG:
                place(i - LAG, d_sb, range(PACK))
            quantise(h_w, h_s, 1, h_b)
            h_b = rounded(cosine)
            if i == 0:
                deal_w3()
            sums[i] = psum.tile([P, PACK, TOK], F32, name="d", bufs=2)
            growth(sums[i], 0, *codes[i])
            if i + 3 < TILES:
                a_banks[i + 3, 0] = angles(i + 3, 0)
            if i + 2 < TILES:
                fracs[i + 2, 0] = reduce_turns(*turns[i + 2, 0])
            if i + 3 < TILES:
                a_banks[i + 3, 1] = angles(i + 3, 1)
        growth(sums[TILES - 1], 1, *codes[TILES - 1])
        spent = [cosine[:, g].rearrange("p j t -> p (j t)").rearrange("p (t j) -> p t j", t=PACK) for g in range(G)]
        early = weigh_growth(TILES - 2, sums[TILES - 2], spent[0][:, :1], slice(0, 1))
        place(TILES - 2, early, range(1))
        d_sb = spent[1]
        for rows in (slice(0, 1), slice(1, PACK)):
            weigh_growth(TILES - 1, sums[TILES - 1], d_sb[:, rows], rows)
        last_wgo = wgo_t[TILES - 1]

        y_rows = out_0.rearrange("(p t) m -> t p m", t=PACK)

        def finish(engine, t, cols):
            y_t = y_all[:, t, :][:, cols]
            engine.tensor_tensor(out=y_t, in0=page[t][:, cols], in1=y_t, op=ALU.mult)
            nc.sync.dma_start(out=y_rows[t][:, cols], in_=y_t)

        place(TILES - 1, d_sb, (0,))
        finish(nc.gpsimd, 0, slice(0, S))
        weigh_growth(TILES - 2, sums[TILES - 2], last_wgo[:, 1:], slice(1, PACK))
        place(TILES - 1, d_sb, (1,))
        place(TILES - 2, last_wgo, (2, 1))
        finish(nc.gpsimd, 1, slice(0, S))
        place(TILES - 2, last_wgo, (3,))
        place(TILES - 1, d_sb, (2, 3))

        quarter = S // 4
        y_w = keep.tile([P, S], U32, name="y_w", align_bytes=64)
        y_s = keep.tile([P, S], U8, name="y_s", align_bytes=64)
        y_b = [keep.tile([P, n * quarter, PACK], BF16, name="y_b%d" % h, align_bytes=64) for h, n in enumerate((2, 1, 1))]
        rounded_q = [y_b[0][:, :quarter], y_b[0][:, quarter:], y_b[1][:], y_b[2][:]]
        y_pairs = out_0.rearrange("(p t) m -> p t m", t=PACK)
        for n, c in enumerate((0, 1, 3, 2)):
            cols = slice(c * quarter, (c + 1) * quarter)
            for t in (2, 3):
                y_t = y_all[:, t, :][:, cols]
                nc.vector.tensor_tensor(out=y_t, in0=page[t][:, cols], in1=y_t, op=ALU.mult)
            if n % 2:
                half = slice(n // 2 * S // 2, (n // 2 + 1) * S // 2)
                nc.sync.dma_start(out=y_pairs[:, 2:, half], in_=y_all[:, 2:, half])
        for c in range(4):
            cols = slice(c * quarter, (c + 1) * quarter)
            copy = nc.vector.tensor_copy if c == 3 else nc.scalar.copy
            copy(
                out=rounded_q[c].rearrange("p (c i) t -> p c t i", i=RUN),
                in_=y_all[:, :, cols].rearrange("p t (c i) -> p c t i", i=RUN),
            )
        for h, lo, hi in ((0, 0, 2), (2, 3, 4), (1, 2, 3)):
            cols = slice(lo * quarter, hi * quarter)
            nc.vector.quantize_mx(
                out=y_w[:, cols].bitcast(FP8X4), scales=y_s[:, cols], in_=y_b[h][:].rearrange("p c t -> p (c t)")
            )
            nc.sync.dma_start(
                out=out_1[0][:, cols, :].rearrange("p c i -> p (c i)").bitcast(I32), in_=y_w[:, cols].bitcast(I32)
            )
        for q in range(QUADS):
            (nc.sync if q % 2 else nc.scalar).dma_start(
                out=out_2[0][4 * q : 4 * q + 4, :].bitcast(I32), in_=y_s[32 * q : 32 * q + 4, :].bitcast(I32)
            )
